import numpy as np
import ml_dtypes


def mxq(x, axis, fmt="e4m3"):
    dtype, down = {"e4m3": (ml_dtypes.float8_e4m3fn, 7), "e5m2": (ml_dtypes.float8_e5m2, 14)}[fmt]
    v = np.moveaxis(np.asarray(x, np.float32).astype(ml_dtypes.bfloat16).astype(np.float64), axis, -1)
    blocks = v.reshape(v.shape[:-1] + (-1, 32))
    amax = np.abs(blocks).max(-1, keepdims=True)
    byte = np.maximum(np.where(amax > 0, np.frexp(amax)[1] - 1 + 127, 0) - down, 1)
    scale = np.exp2(byte - 127.0)
    codes = (blocks / scale).astype(np.float32).astype(dtype).astype(np.float64)
    return np.moveaxis((codes * scale).reshape(v.shape), -1, axis)


WIDE = False


def mx_kscale(k):
    if not WIDE:
        return np.ones(k)
    levels = np.array([10, -10, 5, -5, 0])
    if k % 512:
        return np.exp2(np.random.permutation(np.resize(levels, k // 32))).repeat(32)
    a = np.empty((k // 512, 16))
    for p in range(k // 512):
        a[p, :8] = np.random.permutation(np.resize(levels, 8))
        for g in range(8):
            far = levels[np.abs(levels - a[p, g]) >= 10]
            a[p, g + 8] = far[np.random.randint(len(far))]
    return np.exp2(a.ravel()).repeat(32)


def f64(x):
    return np.asarray(x).astype(np.float64)


def striped(idx):
    return np.tile(idx.reshape(-1, 16).T, (8, 1)).astype(np.uint16)


def unstriped(offs):
    return offs[:16].T.reshape(-1).astype(np.int64)


E2M1 = np.array([0.0, 0.5, 1.0, 1.5, 2.0, 3.0, 4.0, 6.0, -0.0, -0.5, -1.0, -1.5, -2.0, -3.0, -4.0, -6.0])


def pack_fp4(w):
    k, n = w.shape
    w = f64(np.asarray(w, np.float32).astype(ml_dtypes.bfloat16)).reshape(k // 32, 32, n)
    amax = np.abs(w).max(1)
    mant, ex = np.frexp(amax / 6.0)
    byte = np.clip(np.where(amax > 0, np.where(mant > 0.5, ex, ex - 1) + 127, 1), 1, 254)
    scaled = (w * np.exp2(127.0 - byte)[:, None, :]).reshape(k, n).astype(np.float32)
    c = np.ascontiguousarray(scaled.reshape(k // 512, 128, 4, n).transpose(0, 1, 3, 2)).astype(ml_dtypes.float4_e2m1fn).view(np.uint8) & 0xF
    words = (c[..., 0::2] | (c[..., 1::2] << 4)).reshape(k // 512, 128, 2 * n)
    return np.ascontiguousarray(words), np.ascontiguousarray(byte.astype(np.uint8).reshape(k // 512, 16, n))


def unpack_fp4(words, scales):
    g, _, n = scales.shape
    words = np.ascontiguousarray(words).reshape(g, 128, n, 2)
    nib = np.empty((g, 128, n, 4), np.uint8)
    nib[..., 0::2] = words & 0xF
    nib[..., 1::2] = words >> 4
    vals = E2M1[nib] * np.repeat(np.exp2(scales.astype(np.float64) - 127.0), 8, axis=1)[..., None]
    return vals.transpose(0, 1, 3, 2).reshape(g * 512, n)


K, T, S, H, N = 512, 2048, 512, 512, 128
P = 2 ** 7


def setup_inputs():
    n = np.random.standard_normal
    s = mx_kscale(K)[:, None]
    u = mx_kscale(H)
    packed_xT = pack_fp4(n((K, T)) * s)
    return {
        "x_words": packed_xT[0],
        "x_scales": packed_xT[1],
        "w1": (n((K, H)) / np.sqrt(K) / s * u).astype(np.float32),
        "w2": (n((H, N)) / np.sqrt(H) / u[:, None]).astype(np.float32),
        "lam": np.tile(np.random.uniform(0.1, 0.9, S), (P, 1)).astype(np.float32),
        "mu": np.tile(np.random.uniform(0.1, 0.9, S), (P, 1)).astype(np.float32),
        "offs": striped(np.random.permutation(T)[:S]),
        "pos1": striped(np.random.permutation(S)),
    }


def reference(x_words, x_scales, w1, w2, lam, mu, offs, pos1):
    xq = unpack_fp4(x_words, x_scales)[:, unstriped(offs)]
    h = mxq(f64(w1), 0, "e4m3").T @ xq
    z = h * f64(lam)[:1] + h[:, unstriped(pos1)] * f64(mu)[:1]
    return mxq(f64(w2), 0, "e4m3").T @ mxq(z, 0, "e4m3")

@@ -1,0 +1,167 @@
+from contextlib import ExitStack
+
+import concourse.mybir as mybir
+from concourse.masks import make_identity
+
+K, T, S, H, N = 512, 2048, 512, 512, 128
+FLOPS = 2 * K * H * S + 2 * H * N * S
+
+F32 = mybir.dt.float32
+BF16 = mybir.dt.bfloat16
+I32 = mybir.dt.int32
+U32 = mybir.dt.uint32
+U16 = mybir.dt.uint16
+U8 = mybir.dt.uint8
+FP8X4 = mybir.dt.float8_e4m3fn_x4
+FP4X4 = mybir.dt.float4_e2m1fn_x4
+MULT = mybir.AluOpType.mult
+ADD = mybir.AluOpType.add
+COPY = mybir.ActivationFunctionType.Copy
+
+P = 128
+NB = S // P
+
+
+def tile_picked_mixup_none_p_kernel(tc, x_words, x_scales, w1, w2, lam, mu, offs, pos1, out):
+    nc = tc.nc
+    with ExitStack() as ctx:
+        keep = ctx.enter_context(tc.tile_pool(name="keep", bufs=1))
+        psum = ctx.enter_context(tc.psum_pool(name="psum", bufs=1))
+
+        offs_sb = keep.tile([P, S // 16], U16, name="offs_sb")
+        pos_sb = keep.tile([P, S // 16], U16, name="pos_sb")
+        words = keep.tile([P, T], U16, name="words", align_bytes=64)
+        scales = keep.tile([P, T], U8, name="scales", align_bytes=64)
+        w1_raw = [keep.tile([P, 4, 256], F32, name="w1_raw%d" % c, align_bytes=64) for c in range(2)]
+        w2_raw = keep.tile([P, 4, N], F32, name="w2_raw", align_bytes=64)
+        shares = keep.tile([P, P], F32, name="shares", align_bytes=64)
+        ident = keep.tile([P, P], F32, name="ident", align_bytes=64)
+
+        nc.gpsimd.memset(scales[:].bitcast(I32), 0)
+        nc.gpsimd.memset(shares[:], 0.0)
+        make_identity(nc, ident[:])
+
+        nc.sync.dma_start(offs_sb[:], offs)
+        for q in range(4):
+            nc.sync.dma_start(scales[32 * q : 32 * q + 4, :].bitcast(I32), x_scales[0, 4 * q : 4 * q + 4, :].bitcast(I32))
+        nc.sync.dma_start(words[:].bitcast(I32), x_words[0].bitcast(I32))
+        w1_rows = w1.rearrange("(p j) c -> p j c", j=4)
+        for c in range(2):
+            nc.sync.dma_start(w1_raw[c][:], w1_rows[:, :, 256 * c : 256 * (c + 1)])
+        nc.sync.dma_start(pos_sb[:], pos1)
+        nc.sync.dma_start(shares[0:NB, :], lam[0].rearrange("(b p) -> b p", p=P))
+        nc.sync.dma_start(shares[NB : 2 * NB, :], mu[0].rearrange("(b p) -> b p", p=P))
+        nc.sync.dma_start(w2_raw[:], w2.rearrange("(p j) n -> p j n", j=4))
+
+        x_codes = keep.tile([P, S], U16, name="x_codes", align_bytes=64)
+        x_scale = keep.tile([P, S], U8, name="x_scale", align_bytes=64)
+        nc.vector.tensor_copy(x_scale[:], scales[:].indirect(offs_sb[:]))
+        nc.vector.tensor_copy(x_codes[:], words[:].indirect(offs_sb[:]))
+
+        w1_bf = [keep.tile([P, 4 * P], BF16, name="w1_bf%d" % m, align_bytes=64) for m in range(4)]
+        w1_codes = [keep.tile([P, P], U32, name="w1_codes%d" % m, align_bytes=64) for m in range(4)]
+        w1_scale = [keep.tile([P, P], U8, name="w1_scale%d" % m, align_bytes=64) for m in range(4)]
+        h_ps = [psum.tile([P, S], F32, name="h_ps%d" % m, tag="a%d" % m) for m in range(4)]
+        h_sb = [keep.tile([P, S], F32, name="h_sb%d" % m, align_bytes=64) for m in range(4)]
+        g_sb = [keep.tile([P, S], F32, name="g_sb%d" % m, align_bytes=64) for m in range(4)]
+
+        def cast_w1(m, copy):
+            c, u = divmod(m, 2)
+            src = w1_raw[c][:].rearrange("p j (a u e) -> p u a j e", u=2, e=2)[:, u]
+            copy(w1_bf[m][:].rearrange("p (a e j) -> p a j e", e=2, j=4), src)
+
+        def first_product(m):
+            nc.vector.quantize_mx(out=w1_codes[m][:].bitcast(FP8X4), scales=w1_scale[m][:], in_=w1_bf[m][:])
+            nc.tensor.matmul_mx(
+                out=h_ps[m][:],
+                lhsT=w1_codes[m][:].bitcast(FP8X4),
+                lhsT_scale=w1_scale[m][:],
+                rhs=x_codes[:].bitcast(FP4X4),
+                rhs_scale=x_scale[:],
+                start=True,
+                stop=True,
+            )
+            nc.scalar.copy(h_sb[m][:], h_ps[m][:])
+
+        cast_w1(0, nc.vector.tensor_copy)
+        cast_w1(1, nc.scalar.copy)
+        first_product(0)
+        first_product(1)
+        cast_w1(2, nc.vector.tensor_copy)
+        cast_w1(3, nc.vector.tensor_copy)
+        first_product(2)
+        first_product(3)
+
+        shares_ps = psum.tile([P, P], F32, name="shares_ps", tag="t3")
+        share_cols = keep.tile([P, 2 * NB], F32, name="share_cols")
+        nc.tensor.transpose(shares_ps[:], shares[:], ident[:])
+        nc.scalar.copy(share_cols[:], shares_ps[:, 0 : 2 * NB])
+
+        def place(m):
+            c, u = divmod(m, 2)
+            return slice(256 * u + P * c, 256 * u + P * (c + 1))
+
+        ht_ps = [psum.tile([P, H], F32, name="ht_ps%d" % b, tag="t%d" % b) for b in range(NB)]
+        own = [keep.tile([P, H], F32, name="own%d" % b, align_bytes=64) for b in range(NB)]
+        for m in range(4):
+            for b in range(NB):
+                nc.tensor.transpose(ht_ps[b][:, place(m)], h_sb[m][:, P * b : P * (b + 1)], ident[:])
+        for b in range(NB):
+            nc.scalar.activation(own[b][:], ht_ps[b][:], COPY, scale=share_cols[:, b : b + 1])
+
+        w2_bf = keep.tile([P, 4 * N], BF16, name="w2_bf", align_bytes=64)
+        w2_codes = keep.tile([P, N], U32, name="w2_codes", align_bytes=64)
+        w2_scale = keep.tile([P, N], U8, name="w2_scale", align_bytes=64)
+        nc.scalar.copy(
+            w2_bf[:].rearrange("p (a e j) -> p a j e", e=4, j=4),
+            w2_raw[:].rearrange("p j (a e) -> p a j e", e=4),
+        )
+
+        gt_ps = [psum.tile([P, H], F32, name="gt_ps%d" % b, tag="a%d" % b) for b in range(NB)]
+
+        def gather(m, half):
+            nc.vector.tensor_copy(g_sb[m][:, 256 * half : 256 * (half + 1)], h_sb[m][:].indirect(pos_sb[:, 16 * half : 16 * (half + 1)]))
+            for b in (2 * half, 2 * half + 1):
+                nc.tensor.transpose(gt_ps[b][:, place(m)], g_sb[m][:, P * b : P * (b + 1)], ident[:])
+
+        for m, half in ((0, 0), (0, 1), (1, 0), (1, 1), (2, 0), (3, 0), (2, 1), (3, 1)):
+            gather(m, half)
+        nc.vector.quantize_mx(out=w2_codes[:].bitcast(FP8X4), scales=w2_scale[:], in_=w2_bf[:])
+
+        zt = [keep.tile([P, H], BF16, name="zt%d" % b, align_bytes=64) for b in range(NB)]
+        z_bf = [keep.tile([P, 4 * P], BF16, name="z_bf%d" % b, align_bytes=64) for b in range(NB)]
+        z_codes = [keep.tile([P, P], U32, name="z_codes%d" % b, align_bytes=64) for b in range(NB)]
+        z_scale = [keep.tile([P, P], U8, name="z_scale%d" % b, align_bytes=64) for b in range(NB)]
+        res = [keep.tile([P, P], F32, name="res%d" % b, align_bytes=64) for b in range(NB)]
+
+        def mix(b):
+            nc.vector.scalar_tensor_tensor(zt[b][:], gt_ps[b][:], share_cols[:, NB + b : NB + b + 1], own[b][:], MULT, ADD)
+            zw_ps = psum.tile([P, 2, P], F32, name="zw_ps%d" % b, tag="t%d" % b)
+            pairs = zt[b][:].bitcast(F32)
+            for u in range(2):
+                nc.tensor.transpose(zw_ps[:, u, :], pairs[:, P * u : P * (u + 1)], ident[:])
+            nc.scalar.copy(z_bf[b][:].bitcast(F32).rearrange("p (j u) -> p j u", u=2), zw_ps[:].rearrange("p u j -> p j u"))
+
+        def second_product(b):
+            nc.vector.quantize_mx(out=z_codes[b][:].bitcast(FP8X4), scales=z_scale[b][:], in_=z_bf[b][:])
+            out_ps = psum.tile([P, P], F32, name="out_ps%d" % b, tag="a%d" % b)
+            nc.tensor.matmul_mx(
+                out=out_ps[:],
+                lhsT=w2_codes[:].bitcast(FP8X4),
+                lhsT_scale=w2_scale[:],
+                rhs=z_codes[b][:].bitcast(FP8X4),
+                rhs_scale=z_scale[b][:],
+                start=True,
+                stop=True,
+            )
+            nc.scalar.copy(res[b][:], out_ps[:])
+            nc.sync.dma_start(out[:, P * b : P * (b + 1)], res[b][:])
+
+        mix(0)
+        mix(1)
+        mix(2)
+        second_product(0)
+        mix(3)
+        second_product(1)
+        second_product(2)
+        second_product(3)

@@ -1,7 +1,6 @@
 from contextlib import ExitStack
 
 import concourse.mybir as mybir
-from concourse.masks import make_identity
 
 K, T, S, H, N = 512, 2048, 512, 512, 128
 FLOPS = 2 * K * H * S + 2 * H * N * S
@@ -32,65 +31,77 @@ def tile_picked_mixup_none_p_kernel(tc, x_words, x_scales, w1, w2, lam, mu, offs
         pos_sb = keep.tile([P, S // 16], U16, name="pos_sb")
         words = keep.tile([P, T], U16, name="words", align_bytes=64)
         scales = keep.tile([P, T], U8, name="scales", align_bytes=64)
-        w1_raw = [keep.tile([P, 4, 256], F32, name="w1_raw%d" % c, align_bytes=64) for c in range(2)]
-        w2_raw = keep.tile([P, 4, N], F32, name="w2_raw", align_bytes=64)
         shares = keep.tile([P, P], F32, name="shares", align_bytes=64)
         ident = keep.tile([P, P], F32, name="ident", align_bytes=64)
 
         nc.gpsimd.memset(scales[:].bitcast(I32), 0)
-        nc.gpsimd.memset(shares[:], 0.0)
-        make_identity(nc, ident[:])
+        zeros = keep.tile([P, P], F32, name="zeros", tag="raw", align_bytes=64)
+        nc.gpsimd.memset(zeros[:], 0.0)
+        nc.gpsimd.affine_select(
+            out=ident[:], in_=zeros[:], pattern=[[-1, P]], compare_op=mybir.AluOpType.not_equal, fill=1.0, base=0, channel_multiplier=1
+        )
+        nc.gpsimd.tensor_scalar(shares[:], ident[:], 1.0, 0.0, MULT, ADD)
 
         nc.sync.dma_start(offs_sb[:], offs)
+        nc.sync.dma_start(pos_sb[:], pos1)
+        nc.sync.dma_start(words[:].bitcast(I32), x_words[0].bitcast(I32))
         for q in range(4):
             nc.sync.dma_start(scales[32 * q : 32 * q + 4, :].bitcast(I32), x_scales[0, 4 * q : 4 * q + 4, :].bitcast(I32))
-        nc.sync.dma_start(words[:].bitcast(I32), x_words[0].bitcast(I32))
+        w_raw = keep.tile([P, 4 * (H + N)], F32, name="w_raw", tag="raw", align_bytes=64)
+        w1_raw = w_raw[:, 0 : 4 * H].rearrange("p (c j n) -> p c j n", c=2, j=4)
+        w2_raw = w_raw[:, 4 * H :].rearrange("p (j n) -> p j n", j=4)
         w1_rows = w1.rearrange("(p j) c -> p j c", j=4)
         for c in range(2):
-            nc.sync.dma_start(w1_raw[c][:], w1_rows[:, :, 256 * c : 256 * (c + 1)])
-        nc.sync.dma_start(pos_sb[:], pos1)
+            nc.sync.dma_start(w1_raw[:, c], w1_rows[:, :, 256 * c : 256 * (c + 1)])
+        nc.sync.dma_start(w2_raw, w2.rearrange("(p j) n -> p j n", j=4))
         nc.sync.dma_start(shares[0:NB, :], lam[0].rearrange("(b p) -> b p", p=P))
         nc.sync.dma_start(shares[NB : 2 * NB, :], mu[0].rearrange("(b p) -> b p", p=P))
-        nc.sync.dma_start(w2_raw[:], w2.rearrange("(p j) n -> p j n", j=4))
 
         x_codes = keep.tile([P, S], U16, name="x_codes", align_bytes=64)
         x_scale = keep.tile([P, S], U8, name="x_scale", align_bytes=64)
-        nc.vector.tensor_copy(x_scale[:], scales[:].indirect(offs_sb[:]))
         nc.vector.tensor_copy(x_codes[:], words[:].indirect(offs_sb[:]))
+        nc.vector.tensor_copy(x_scale[:], scales[:].indirect(offs_sb[:]))
 
-        w1_bf = [keep.tile([P, 4 * P], BF16, name="w1_bf%d" % m, align_bytes=64) for m in range(4)]
-        w1_codes = [keep.tile([P, P], U32, name="w1_codes%d" % m, align_bytes=64) for m in range(4)]
-        w1_scale = [keep.tile([P, P], U8, name="w1_scale%d" % m, align_bytes=64) for m in range(4)]
-        h_ps = [psum.tile([P, S], F32, name="h_ps%d" % m, tag="a%d" % m) for m in range(4)]
+        w1_codes = keep.tile([P, 4 * P], U32, name="w1_codes", align_bytes=64)
+        w1_scale = keep.tile([P, 4 * P], U8, name="w1_scale", align_bytes=64)
         h_sb = [keep.tile([P, S], F32, name="h_sb%d" % m, align_bytes=64) for m in range(4)]
         g_sb = [keep.tile([P, S], F32, name="g_sb%d" % m, align_bytes=64) for m in range(4)]
 
-        def cast_w1(m, copy):
-            c, u = divmod(m, 2)
-            src = w1_raw[c][:].rearrange("p j (a u e) -> p u a j e", u=2, e=2)[:, u]
-            copy(w1_bf[m][:].rearrange("p (a e j) -> p a j e", e=2, j=4), src)
+        def cast_w1(c, us, tag, copy):
+            staged = keep.tile([P, len(us) * 4 * P], BF16, name="w1_bf%d_%d" % (c, us[0]), tag=tag, align_bytes=64)
+            src = w1_raw[:, c].rearrange("p j (a u e) -> p a j u e", u=2, e=2)[:, :, :, us[0] : us[-1] + 1]
+            copy(staged[:].rearrange("p (u a e j) -> p a j u e", u=len(us), e=2, j=4), src)
+            return staged
 
-        def first_product(m):
-            nc.vector.quantize_mx(out=w1_codes[m][:].bitcast(FP8X4), scales=w1_scale[m][:], in_=w1_bf[m][:])
+        def quantize_w1(m, staged):
+            cols = slice(P * m, P * m + staged.shape[1] // 4)
+            nc.vector.quantize_mx(out=w1_codes[:, cols].bitcast(FP8X4), scales=w1_scale[:, cols], in_=staged[:])
+
+        def first_product(m, half):
+            cols = slice(256 * half, 256 * (half + 1))
+            bank = psum.tile([P, 256], F32, name="h_ps%d_%d" % (m, half), tag="a%d" % (2 * (m % 2) + half))
             nc.tensor.matmul_mx(
-                out=h_ps[m][:],
-                lhsT=w1_codes[m][:].bitcast(FP8X4),
-                lhsT_scale=w1_scale[m][:],
-                rhs=x_codes[:].bitcast(FP4X4),
-                rhs_scale=x_scale[:],
+                out=bank[:],
+                lhsT=w1_codes[:, P * m : P * (m + 1)].bitcast(FP8X4),
+                lhsT_scale=w1_scale[:, P * m : P * (m + 1)],
+                rhs=x_codes[:, cols].bitcast(FP4X4),
+                rhs_scale=x_scale[:, cols],
                 start=True,
                 stop=True,
             )
-            nc.scalar.copy(h_sb[m][:], h_ps[m][:])
+            nc.scalar.copy(h_sb[m][:, cols], bank[:])
 
-        cast_w1(0, nc.vector.tensor_copy)
-        cast_w1(1, nc.scalar.copy)
-        first_product(0)
-        first_product(1)
-        cast_w1(2, nc.vector.tensor_copy)
-        cast_w1(3, nc.vector.tensor_copy)
-        first_product(2)
-        first_product(3)
+        staged0 = cast_w1(0, [0], "w1_bf_a", nc.scalar.copy)
+        staged1 = cast_w1(0, [1], "w1_bf_b", nc.scalar.copy)
+        quantize_w1(0, staged0)
+        first_product(0, 0)
+        first_product(0, 1)
+        staged23 = cast_w1(1, [0, 1], "w1_bf_a", nc.vector.tensor_copy)
+        quantize_w1(1, staged1)
+        quantize_w1(2, staged23)
+        for m in range(1, 4):
+            first_product(m, 0)
+            first_product(m, 1)
 
         shares_ps = psum.tile([P, P], F32, name="shares_ps", tag="t3")
         share_cols = keep.tile([P, 2 * NB], F32, name="share_cols")
@@ -114,17 +125,17 @@ def tile_picked_mixup_none_p_kernel(tc, x_words, x_scales, w1, w2, lam, mu, offs
         w2_scale = keep.tile([P, N], U8, name="w2_scale", align_bytes=64)
         nc.scalar.copy(
             w2_bf[:].rearrange("p (a e j) -> p a j e", e=4, j=4),
-            w2_raw[:].rearrange("p j (a e) -> p a j e", e=4),
+            w2_raw.rearrange("p j (a e) -> p a j e", e=4),
         )
 
-        gt_ps = [psum.tile([P, H], F32, name="gt_ps%d" % b, tag="a%d" % b) for b in range(NB)]
+        gt_ps = [psum.tile([P, H], F32, name="gt_ps%d" % b, tag="a%d" % ((b + 2) % 4)) for b in range(NB)]
 
         def gather(m, half):
             nc.vector.tensor_copy(g_sb[m][:, 256 * half : 256 * (half + 1)], h_sb[m][:].indirect(pos_sb[:, 16 * half : 16 * (half + 1)]))
             for b in (2 * half, 2 * half + 1):
                 nc.tensor.transpose(gt_ps[b][:, place(m)], g_sb[m][:, P * b : P * (b + 1)], ident[:])
 
-        for m, half in ((0, 0), (0, 1), (1, 0), (1, 1), (2, 0), (3, 0), (2, 1), (3, 1)):
+        for m, half in ((0, 1), (0, 0), (1, 1), (1, 0), (2, 0), (2, 1), (3, 0), (3, 1)):
             gather(m, half)
         nc.vector.quantize_mx(out=w2_codes[:].bitcast(FP8X4), scales=w2_scale[:], in_=w2_bf[:])
 
@@ -144,7 +155,7 @@ def tile_picked_mixup_none_p_kernel(tc, x_words, x_scales, w1, w2, lam, mu, offs
 
         def second_product(b):
             nc.vector.quantize_mx(out=z_codes[b][:].bitcast(FP8X4), scales=z_scale[b][:], in_=z_bf[b][:])
-            out_ps = psum.tile([P, P], F32, name="out_ps%d" % b, tag="a%d" % b)
+            out_ps = psum.tile([P, P], F32, name="out_ps%d" % b, tag="a%d" % ((b + 2) % 4))
             nc.tensor.matmul_mx(
                 out=out_ps[:],
                 lhsT=w2_codes[:].bitcast(FP8X4),

@@ -43,8 +43,8 @@ def tile_picked_mixup_none_p_kernel(tc, x_words, x_scales, w1, w2, lam, mu, offs
         nc.gpsimd.tensor_scalar(shares[:], ident[:], 1.0, 0.0, MULT, ADD)
 
         nc.sync.dma_start(offs_sb[:], offs)
-        nc.sync.dma_start(pos_sb[:], pos1)
         nc.sync.dma_start(words[:].bitcast(I32), x_words[0].bitcast(I32))
+        nc.sync.dma_start(pos_sb[:], pos1)
         for q in range(4):
             nc.sync.dma_start(scales[32 * q : 32 * q + 4, :].bitcast(I32), x_scales[0, 4 * q : 4 * q + 4, :].bitcast(I32))
         w_raw = keep.tile([P, 4 * (H + N)], F32, name="w_raw", tag="raw", align_bytes=64)
@@ -64,7 +64,8 @@ def tile_picked_mixup_none_p_kernel(tc, x_words, x_scales, w1, w2, lam, mu, offs
 
         w1_codes = keep.tile([P, 4 * P], U32, name="w1_codes", align_bytes=64)
         w1_scale = keep.tile([P, 4 * P], U8, name="w1_scale", align_bytes=64)
-        h_sb = [keep.tile([P, S], F32, name="h_sb%d" % m, align_bytes=64) for m in range(4)]
+        h_all = keep.tile([P, 4 * S], F32, name="h_all", align_bytes=64)
+        h_sb = [h_all[:, S * (3 - m) : S * (4 - m)] for m in range(4)]
         g_sb = [keep.tile([P, S], F32, name="g_sb%d" % m, align_bytes=64) for m in range(4)]
 
         def cast_w1(c, us, tag, copy):
@@ -113,15 +114,31 @@ def tile_picked_mixup_none_p_kernel(tc, x_words, x_scales, w1, w2, lam, mu, offs
             return slice(256 * u + P * c, 256 * u + P * (c + 1))
 
         ht_ps = [psum.tile([P, H], F32, name="ht_ps%d" % b, tag="t%d" % b) for b in range(NB)]
-        own = [keep.tile([P, H], F32, name="own%d" % b, align_bytes=64) for b in range(NB)]
+        own = [keep.tile([P, H], F32, name="own%d" % b, align_bytes=64) for b in range(NB - 1)]
+        own_last = [keep.tile([P, H // 2], F32, name="own_last%d" % u, tag="own_last%d" % u, align_bytes=64) for u in range(2)]
         for m in range(4):
             for b in range(NB):
                 nc.tensor.transpose(ht_ps[b][:, place(m)], h_sb[m][:, P * b : P * (b + 1)], ident[:])
-        for b in range(NB):
+        z0_ps = psum.tile([P, 4, P], F32, name="z0_ps", tag="t0")
+
+        def scale_slots(dst, src, share):
+            nc.scalar.activation(
+                dst.rearrange("p (u e w) -> p u e w", u=2, e=2), src.rearrange("p (u w e) -> p u e w", u=2, e=2), COPY, scale=share
+            )
+
+        def add_slots(src, first, last):
+            for t in range(4):
+                nc.tensor.matmul(
+                    z0_ps[:, t, :], src[:, P * t : P * (t + 1)], ident[:], start=first and t == 0, stop=last and t == 3, is_transpose=True
+                )
+
+        scale_slots(own[0][:], ht_ps[0][:], share_cols[:, 0:1])
+        for b in range(1, NB - 1):
             nc.scalar.activation(own[b][:], ht_ps[b][:], COPY, scale=share_cols[:, b : b + 1])
+        for u in range(2):
+            nc.scalar.activation(own_last[u][:], ht_ps[3][:, 256 * u : 256 * (u + 1)], COPY, scale=share_cols[:, 3:4])
 
         w2_bf = keep.tile([P, 4 * N], BF16, name="w2_bf", align_bytes=64)
-        w2_codes = keep.tile([P, N], U32, name="w2_codes", align_bytes=64)
         w2_scale = keep.tile([P, N], U8, name="w2_scale", align_bytes=64)
         nc.scalar.copy(
             w2_bf[:].rearrange("p (a e j) -> p a j e", e=4, j=4),
@@ -130,30 +147,49 @@ def tile_picked_mixup_none_p_kernel(tc, x_words, x_scales, w1, w2, lam, mu, offs
 
         gt_ps = [psum.tile([P, H], F32, name="gt_ps%d" % b, tag="a%d" % ((b + 2) % 4)) for b in range(NB)]
 
-        def gather(m, half):
-            nc.vector.tensor_copy(g_sb[m][:, 256 * half : 256 * (half + 1)], h_sb[m][:].indirect(pos_sb[:, 16 * half : 16 * (half + 1)]))
-            for b in (2 * half, 2 * half + 1):
+        def gather(m, first, last):
+            cols = slice(P * first, P * last)
+            width = S if last - first < NB else 2 * S
+            window = h_all[:, S * (3 - m) : S * (3 - m) + width]
+            nc.vector.tensor_copy(g_sb[m][:, cols], window.indirect(pos_sb[:, 8 * first : 8 * last]))
+            for b in range(first, last):
                 nc.tensor.transpose(gt_ps[b][:, place(m)], g_sb[m][:, P * b : P * (b + 1)], ident[:])
 
-        for m, half in ((0, 1), (0, 0), (1, 1), (1, 0), (2, 0), (2, 1), (3, 0), (3, 1)):
-            gather(m, half)
-        nc.vector.quantize_mx(out=w2_codes[:].bitcast(FP8X4), scales=w2_scale[:], in_=w2_bf[:])
+        gather(0, 2, 4)
+        gather(0, 0, 2)
+        add_slots(own[0], True, False)
+        gather(1, 2, 4)
+        gather(1, 0, 2)
+        gather(2, 0, 4)
+        gather(3, 0, 2)
+        gather(3, 2, 4)
 
-        zt = [keep.tile([P, H], BF16, name="zt%d" % b, align_bytes=64) for b in range(NB)]
-        z_bf = [keep.tile([P, 4 * P], BF16, name="z_bf%d" % b, align_bytes=64) for b in range(NB)]
-        z_codes = [keep.tile([P, P], U32, name="z_codes%d" % b, align_bytes=64) for b in range(NB)]
+        zt = {b: keep.tile([P, H], BF16, name="zt%d" % b, align_bytes=64) for b in range(1, NB)}
+        partner = keep.tile([P, H], F32, name="partner", align_bytes=64)
+        z_bf = {}
+        code_tags = ["z_codes0", "z_codes1", "z_codes2", "z_codes3"]
+        z_codes = {}
         z_scale = [keep.tile([P, P], U8, name="z_scale%d" % b, align_bytes=64) for b in range(NB)]
         res = [keep.tile([P, P], F32, name="res%d" % b, align_bytes=64) for b in range(NB)]
 
-        def mix(b):
-            nc.vector.scalar_tensor_tensor(zt[b][:], gt_ps[b][:], share_cols[:, NB + b : NB + b + 1], own[b][:], MULT, ADD)
-            zw_ps = psum.tile([P, 2, P], F32, name="zw_ps%d" % b, tag="t%d" % b)
-            pairs = zt[b][:].bitcast(F32)
-            for u in range(2):
-                nc.tensor.transpose(zw_ps[:, u, :], pairs[:, P * u : P * (u + 1)], ident[:])
-            nc.scalar.copy(z_bf[b][:].bitcast(F32).rearrange("p (j u) -> p j u", u=2), zw_ps[:].rearrange("p u j -> p j u"))
+        zw_ps = {}
 
-        def second_product(b):
+        def mix(b, pieces):
+            zw_ps[b] = psum.tile([P, 2, P], F32, name="zw_ps%d" % b, tag="t%d" % b)
+            pairs = zt[b][:].bitcast(F32)
+            width = H // len(pieces)
+            for n, piece in enumerate(pieces):
+                cols = slice(width * n, width * (n + 1))
+                nc.vector.scalar_tensor_tensor(zt[b][:, cols], gt_ps[b][:, cols], share_cols[:, NB + b : NB + b + 1], piece[:], MULT, ADD)
+            for u in range(2):
+                nc.tensor.transpose(zw_ps[b][:, u, :], pairs[:, P * u : P * (u + 1)], ident[:])
+
+        def interleave(b, tag, copy):
+            z_bf[b] = keep.tile([P, 4 * P], BF16, name="z_bf%d" % b, tag=tag, align_bytes=64)
+            copy(z_bf[b][:].bitcast(F32).rearrange("p (j u) -> p j u", u=2), zw_ps[b][:].rearrange("p u j -> p j u"))
+
+        def second_product(b, copy):
+            z_codes[b] = keep.tile([P, P], U32, name="z_codes%d" % b, tag=code_tags[b], align_bytes=64)
             nc.vector.quantize_mx(out=z_codes[b][:].bitcast(FP8X4), scales=z_scale[b][:], in_=z_bf[b][:])
             out_ps = psum.tile([P, P], F32, name="out_ps%d" % b, tag="a%d" % ((b + 2) % 4))
             nc.tensor.matmul_mx(
@@ -165,14 +201,22 @@ def tile_picked_mixup_none_p_kernel(tc, x_words, x_scales, w1, w2, lam, mu, offs
                 start=True,
                 stop=True,
             )
-            nc.scalar.copy(res[b][:], out_ps[:])
+            copy(res[b][:], out_ps[:])
             nc.sync.dma_start(out[:, P * b : P * (b + 1)], res[b][:])
 
-        mix(0)
-        mix(1)
-        mix(2)
-        second_product(0)
-        mix(3)
-        second_product(1)
-        second_product(2)
-        second_product(3)
+        scale_slots(partner[:], gt_ps[0][:], share_cols[:, NB : NB + 1])
+        mix(1, [own[1]])
+        add_slots(partner, False, True)
+        interleave(1, "z_bf1", nc.scalar.copy)
+        z_bf[0] = keep.tile([P, 4 * P], BF16, name="z_bf0", align_bytes=64)
+        nc.scalar.copy(z_bf[0][:].rearrange("p (j t) -> p j t", t=4), z0_ps[:].rearrange("p t j -> p j t"))
+        mix(2, [own[2]])
+        mix(3, own_last)
+        w2_codes = keep.tile([P, N], U32, name="w2_codes", tag="own_last0", align_bytes=64)
+        nc.vector.quantize_mx(out=w2_codes[:].bitcast(FP8X4), scales=w2_scale[:], in_=w2_bf[:])
+        interleave(3, "z_bf3", nc.scalar.copy)
+        interleave(2, "own_last1", nc.vector.tensor_copy)
+        second_product(1, nc.vector.tensor_copy)
+        second_product(0, nc.vector.tensor_copy)
+        second_product(2, nc.scalar.copy)
+        second_product(3, nc.scalar.copy)

@@ -19,6 +19,7 @@ COPY = mybir.ActivationFunctionType.Copy
 
 P = 128
 NB = S // P
+HALF = S // 2
 
 
 def tile_picked_mixup_none_p_kernel(tc, x_words, x_scales, w1, w2, lam, mu, offs, pos1, out):
@@ -31,7 +32,7 @@ def tile_picked_mixup_none_p_kernel(tc, x_words, x_scales, w1, w2, lam, mu, offs
         pos_sb = keep.tile([P, S // 16], U16, name="pos_sb")
         words = keep.tile([P, T], U16, name="words", align_bytes=64)
         scales = keep.tile([P, T], U8, name="scales", align_bytes=64)
-        shares = keep.tile([P, P], F32, name="shares", align_bytes=64)
+        lam_rows = keep.tile([P, P], F32, name="lam_rows", align_bytes=64)
         ident = keep.tile([P, P], F32, name="ident", align_bytes=64)
 
         nc.gpsimd.memset(scales[:].bitcast(I32), 0)
@@ -40,158 +41,120 @@ def tile_picked_mixup_none_p_kernel(tc, x_words, x_scales, w1, w2, lam, mu, offs
         nc.gpsimd.affine_select(
             out=ident[:], in_=zeros[:], pattern=[[-1, P]], compare_op=mybir.AluOpType.not_equal, fill=1.0, base=0, channel_multiplier=1
         )
-        nc.gpsimd.tensor_scalar(shares[:], ident[:], 1.0, 0.0, MULT, ADD)
+        nc.gpsimd.tensor_scalar(lam_rows[:], ident[:], 1.0, 0.0, MULT, ADD)
 
         nc.sync.dma_start(offs_sb[:], offs)
         nc.sync.dma_start(words[:].bitcast(I32), x_words[0].bitcast(I32))
         nc.sync.dma_start(pos_sb[:], pos1)
         for q in range(4):
             nc.sync.dma_start(scales[32 * q : 32 * q + 4, :].bitcast(I32), x_scales[0, 4 * q : 4 * q + 4, :].bitcast(I32))
-        w_raw = keep.tile([P, 4 * (H + N)], F32, name="w_raw", tag="raw", align_bytes=64)
-        w1_raw = w_raw[:, 0 : 4 * H].rearrange("p (c j n) -> p c j n", c=2, j=4)
-        w2_raw = w_raw[:, 4 * H :].rearrange("p (j n) -> p j n", j=4)
+        raw = keep.tile([P, 4 * (H + N) + S], F32, name="raw", tag="raw", align_bytes=64)
+        w1_raw = raw[:, 0 : 4 * H].rearrange("p (c j n) -> p c j n", c=2, j=4)
+        w2_raw = raw[:, 4 * H : 4 * (H + N)].rearrange("p (j n) -> p j n", j=4)
+        mu_sb = raw[:, 4 * (H + N) :]
         w1_rows = w1.rearrange("(p j) c -> p j c", j=4)
         for c in range(2):
             nc.sync.dma_start(w1_raw[:, c], w1_rows[:, :, 256 * c : 256 * (c + 1)])
         nc.sync.dma_start(w2_raw, w2.rearrange("(p j) n -> p j n", j=4))
-        nc.sync.dma_start(shares[0:NB, :], lam[0].rearrange("(b p) -> b p", p=P))
-        nc.sync.dma_start(shares[NB : 2 * NB, :], mu[0].rearrange("(b p) -> b p", p=P))
+        nc.sync.dma_start(mu_sb, mu)
+        nc.sync.dma_start(lam_rows[0:NB, :], lam[0].rearrange("(b p) -> b p", p=P))
 
         x_codes = keep.tile([P, S], U16, name="x_codes", align_bytes=64)
         x_scale = keep.tile([P, S], U8, name="x_scale", align_bytes=64)
         nc.vector.tensor_copy(x_codes[:], words[:].indirect(offs_sb[:]))
         nc.vector.tensor_copy(x_scale[:], scales[:].indirect(offs_sb[:]))
 
+        w1_bf = [keep.tile([P, 2, P * 4], BF16, name="w1_bf%d" % u, align_bytes=64) for u in range(2)]
         w1_codes = keep.tile([P, 4 * P], U32, name="w1_codes", align_bytes=64)
         w1_scale = keep.tile([P, 4 * P], U8, name="w1_scale", align_bytes=64)
-        h_all = keep.tile([P, 4 * S], F32, name="h_all", align_bytes=64)
-        h_sb = [h_all[:, S * (3 - m) : S * (4 - m)] for m in range(4)]
-        g_sb = [keep.tile([P, S], F32, name="g_sb%d" % m, align_bytes=64) for m in range(4)]
+        h_sb = [keep.tile([P, S], F32, name="h_sb%d" % t, align_bytes=64) for t in range(4)]
+        partner = keep.tile([P, 4, S], F32, name="partner", align_bytes=64)
 
-        def cast_w1(c, us, tag, copy):
-            staged = keep.tile([P, len(us) * 4 * P], BF16, name="w1_bf%d_%d" % (c, us[0]), tag=tag, align_bytes=64)
-            src = w1_raw[:, c].rearrange("p j (a u e) -> p a j u e", u=2, e=2)[:, :, :, us[0] : us[-1] + 1]
-            copy(staged[:].rearrange("p (u a e j) -> p a j u e", u=len(us), e=2, j=4), src)
-            return staged
+        def cast_w1(c, u, copy):
+            src = w1_raw[:, c].rearrange("p j (m u e) -> p u m j e", u=2, e=2)[:, u]
+            dst = w1_bf[u][:].rearrange("p e (c m j) -> p c m j e", c=2, j=4)[:, c]
+            copy(dst, src)
 
-        def quantize_w1(m, staged):
-            cols = slice(P * m, P * m + staged.shape[1] // 4)
-            nc.vector.quantize_mx(out=w1_codes[:, cols].bitcast(FP8X4), scales=w1_scale[:, cols], in_=staged[:])
+        def quantize_w1(first, last):
+            cols = slice(P * first, P * last)
+            u = first // 2
+            staged = w1_bf[u][:, first - 2 * u : last - 2 * u, :].rearrange("p e w -> p (e w)")
+            nc.vector.quantize_mx(out=w1_codes[:, cols].bitcast(FP8X4), scales=w1_scale[:, cols], in_=staged)
 
-        def first_product(m, half):
-            cols = slice(256 * half, 256 * (half + 1))
-            bank = psum.tile([P, 256], F32, name="h_ps%d_%d" % (m, half), tag="a%d" % (2 * (m % 2) + half))
+        def first_product(t, half, copy):
+            cols = slice(HALF * half, HALF * (half + 1))
+            bank = psum.tile([P, HALF], F32, name="h_ps%d_%d" % (t, half), tag="a%d" % (2 * (t % 2) + half))
             nc.tensor.matmul_mx(
                 out=bank[:],
-                lhsT=w1_codes[:, P * m : P * (m + 1)].bitcast(FP8X4),
-                lhsT_scale=w1_scale[:, P * m : P * (m + 1)],
+                lhsT=w1_codes[:, P * t : P * (t + 1)].bitcast(FP8X4),
+                lhsT_scale=w1_scale[:, P * t : P * (t + 1)],
                 rhs=x_codes[:, cols].bitcast(FP4X4),
                 rhs_scale=x_scale[:, cols],
                 start=True,
                 stop=True,
             )
-            nc.scalar.copy(h_sb[m][:, cols], bank[:])
+            copy(h_sb[t][:, cols], bank[:])
 
-        staged0 = cast_w1(0, [0], "w1_bf_a", nc.scalar.copy)
-        staged1 = cast_w1(0, [1], "w1_bf_b", nc.scalar.copy)
-        quantize_w1(0, staged0)
-        first_product(0, 0)
-        first_product(0, 1)
-        staged23 = cast_w1(1, [0, 1], "w1_bf_a", nc.vector.tensor_copy)
-        quantize_w1(1, staged1)
-        quantize_w1(2, staged23)
-        for m in range(1, 4):
-            first_product(m, 0)
-            first_product(m, 1)
+        cast_w1(0, 0, nc.scalar.copy)
+        cast_w1(0, 1, nc.scalar.copy)
+        cast_w1(1, 0, nc.vector.tensor_copy)
+        cast_w1(1, 1, nc.scalar.copy)
+        quantize_w1(0, 1)
+        quantize_w1(1, 2)
+        quantize_w1(2, 4)
+        for t in range(4):
+            first_product(t, 0, nc.scalar.copy)
+            first_product(t, 1, nc.scalar.copy)
 
-        shares_ps = psum.tile([P, P], F32, name="shares_ps", tag="t3")
-        share_cols = keep.tile([P, 2 * NB], F32, name="share_cols")
-        nc.tensor.transpose(shares_ps[:], shares[:], ident[:])
-        nc.scalar.copy(share_cols[:], shares_ps[:, 0 : 2 * NB])
-
-        def place(m):
-            c, u = divmod(m, 2)
-            return slice(256 * u + P * c, 256 * u + P * (c + 1))
-
-        ht_ps = [psum.tile([P, H], F32, name="ht_ps%d" % b, tag="t%d" % b) for b in range(NB)]
-        own = [keep.tile([P, H], F32, name="own%d" % b, align_bytes=64) for b in range(NB - 1)]
-        own_last = [keep.tile([P, H // 2], F32, name="own_last%d" % u, tag="own_last%d" % u, align_bytes=64) for u in range(2)]
-        for m in range(4):
-            for b in range(NB):
-                nc.tensor.transpose(ht_ps[b][:, place(m)], h_sb[m][:, P * b : P * (b + 1)], ident[:])
-        z0_ps = psum.tile([P, 4, P], F32, name="z0_ps", tag="t0")
-
-        def scale_slots(dst, src, share):
-            nc.scalar.activation(
-                dst.rearrange("p (u e w) -> p u e w", u=2, e=2), src.rearrange("p (u w e) -> p u e w", u=2, e=2), COPY, scale=share
-            )
-
-        def add_slots(src, first, last):
-            for t in range(4):
-                nc.tensor.matmul(
-                    z0_ps[:, t, :], src[:, P * t : P * (t + 1)], ident[:], start=first and t == 0, stop=last and t == 3, is_transpose=True
-                )
-
-        scale_slots(own[0][:], ht_ps[0][:], share_cols[:, 0:1])
-        for b in range(1, NB - 1):
-            nc.scalar.activation(own[b][:], ht_ps[b][:], COPY, scale=share_cols[:, b : b + 1])
-        for u in range(2):
-            nc.scalar.activation(own_last[u][:], ht_ps[3][:, 256 * u : 256 * (u + 1)], COPY, scale=share_cols[:, 3:4])
-
-        w2_bf = keep.tile([P, 4 * N], BF16, name="w2_bf", align_bytes=64)
+        w2_bf = keep.tile([P, 4 * N], BF16, name="w2_bf", tag="w1_bf1", align_bytes=64)
+        w2_codes = keep.tile([P, N], U32, name="w2_codes", align_bytes=64)
         w2_scale = keep.tile([P, N], U8, name="w2_scale", align_bytes=64)
-        nc.scalar.copy(
+        nc.vector.tensor_copy(
             w2_bf[:].rearrange("p (a e j) -> p a j e", e=4, j=4),
             w2_raw.rearrange("p j (a e) -> p a j e", e=4),
         )
 
-        gt_ps = [psum.tile([P, H], F32, name="gt_ps%d" % b, tag="a%d" % ((b + 2) % 4)) for b in range(NB)]
+        nc.vector.quantize_mx(out=w2_codes[:].bitcast(FP8X4), scales=w2_scale[:], in_=w2_bf[:])
 
-        def gather(m, first, last):
-            cols = slice(P * first, P * last)
-            width = S if last - first < NB else 2 * S
-            window = h_all[:, S * (3 - m) : S * (3 - m) + width]
-            nc.vector.tensor_copy(g_sb[m][:, cols], window.indirect(pos_sb[:, 8 * first : 8 * last]))
-            for b in range(first, last):
-                nc.tensor.transpose(gt_ps[b][:, place(m)], g_sb[m][:, P * b : P * (b + 1)], ident[:])
+        lam_ps = psum.tile([P, P], F32, name="lam_ps", tag="a0")
+        lam_cols = keep.tile([P, NB], F32, name="lam_cols")
+        nc.tensor.transpose(lam_ps[:], lam_rows[:], ident[:])
+        nc.scalar.copy(lam_cols[:], lam_ps[:, 0:NB])
 
-        gather(0, 2, 4)
-        gather(0, 0, 2)
-        add_slots(own[0], True, False)
-        gather(1, 2, 4)
-        gather(1, 0, 2)
-        gather(2, 0, 4)
-        gather(3, 0, 2)
-        gather(3, 2, 4)
+        ht_ps = [psum.tile([P, 4, P], F32, name="ht_ps%d" % b, tag="t%d" % b) for b in range(NB)]
+        for t in range(4):
+            for b in range(NB):
+                nc.tensor.transpose(ht_ps[b][:, t, :], h_sb[t][:, P * b : P * (b + 1)], ident[:])
+        own_t = [keep.tile([P, 4, P], F32, name="own_t%d" % b, align_bytes=64) for b in range(NB)]
+        own_ps = [psum.tile([P, 4, P], F32, name="own_ps%d" % b, tag="a%d" % b) for b in range(NB)]
+        for b in range(NB):
+            nc.scalar.activation(own_t[b][:], ht_ps[b][:], COPY, scale=lam_cols[:, b : b + 1])
+            for t in range(4):
+                nc.tensor.transpose(own_ps[b][:, t, :], own_t[b][:, t, :], ident[:])
 
-        zt = {b: keep.tile([P, H], BF16, name="zt%d" % b, align_bytes=64) for b in range(1, NB)}
-        partner = keep.tile([P, H], F32, name="partner", align_bytes=64)
-        z_bf = {}
-        code_tags = ["z_codes0", "z_codes1", "z_codes2", "z_codes3"]
-        z_codes = {}
+        for t in range(4):
+            for half in range(2):
+                cols = slice(HALF * half, HALF * (half + 1))
+                nc.vector.tensor_tensor(
+                    partner[:, t, cols], h_sb[t][:].indirect(pos_sb[:, 16 * half : 16 * (half + 1)]), mu_sb[:, cols], MULT
+                )
+
+        z_bf = [keep.tile([P, 4 * P], BF16, name="z_bf%d" % b, align_bytes=64) for b in range(NB)]
+        z_codes = [keep.tile([P, P], U32, name="z_codes%d" % b, align_bytes=64) for b in range(NB)]
         z_scale = [keep.tile([P, P], U8, name="z_scale%d" % b, align_bytes=64) for b in range(NB)]
         res = [keep.tile([P, P], F32, name="res%d" % b, align_bytes=64) for b in range(NB)]
 
-        zw_ps = {}
+        def mix(b):
+            nc.vector.tensor_tensor(
+                z_bf[b][:].rearrange("p (q i t) -> p q t i", i=2, t=4),
+                own_ps[b][:].rearrange("p t (q i) -> p q t i", i=2),
+                partner[:, :, P * b : P * (b + 1)].rearrange("p t (q i) -> p q t i", i=2),
+                ADD,
+            )
 
-        def mix(b, pieces):
-            zw_ps[b] = psum.tile([P, 2, P], F32, name="zw_ps%d" % b, tag="t%d" % b)
-            pairs = zt[b][:].bitcast(F32)
-            width = H // len(pieces)
-            for n, piece in enumerate(pieces):
-                cols = slice(width * n, width * (n + 1))
-                nc.vector.scalar_tensor_tensor(zt[b][:, cols], gt_ps[b][:, cols], share_cols[:, NB + b : NB + b + 1], piece[:], MULT, ADD)
-            for u in range(2):
-                nc.tensor.transpose(zw_ps[b][:, u, :], pairs[:, P * u : P * (u + 1)], ident[:])
-
-        def interleave(b, tag, copy):
-            z_bf[b] = keep.tile([P, 4 * P], BF16, name="z_bf%d" % b, tag=tag, align_bytes=64)
-            copy(z_bf[b][:].bitcast(F32).rearrange("p (j u) -> p j u", u=2), zw_ps[b][:].rearrange("p u j -> p j u"))
-
-        def second_product(b, copy):
-            z_codes[b] = keep.tile([P, P], U32, name="z_codes%d" % b, tag=code_tags[b], align_bytes=64)
+        def second_product(b):
             nc.vector.quantize_mx(out=z_codes[b][:].bitcast(FP8X4), scales=z_scale[b][:], in_=z_bf[b][:])
-            out_ps = psum.tile([P, P], F32, name="out_ps%d" % b, tag="a%d" % ((b + 2) % 4))
+            out_ps = psum.tile([P, P], F32, name="out_ps%d" % b, tag="t%d" % b)
             nc.tensor.matmul_mx(
                 out=out_ps[:],
                 lhsT=w2_codes[:].bitcast(FP8X4),
@@ -201,22 +164,14 @@ def tile_picked_mixup_none_p_kernel(tc, x_words, x_scales, w1, w2, lam, mu, offs
                 start=True,
                 stop=True,
             )
-            copy(res[b][:], out_ps[:])
+            nc.scalar.copy(res[b][:], out_ps[:])
             nc.sync.dma_start(out[:, P * b : P * (b + 1)], res[b][:])
 
-        scale_slots(partner[:], gt_ps[0][:], share_cols[:, NB : NB + 1])
-        mix(1, [own[1]])
-        add_slots(partner, False, True)
-        interleave(1, "z_bf1", nc.scalar.copy)
-        z_bf[0] = keep.tile([P, 4 * P], BF16, name="z_bf0", align_bytes=64)
-        nc.scalar.copy(z_bf[0][:].rearrange("p (j t) -> p j t", t=4), z0_ps[:].rearrange("p t j -> p j t"))
-        mix(2, [own[2]])
-        mix(3, own_last)
-        w2_codes = keep.tile([P, N], U32, name="w2_codes", tag="own_last0", align_bytes=64)
-        nc.vector.quantize_mx(out=w2_codes[:].bitcast(FP8X4), scales=w2_scale[:], in_=w2_bf[:])
-        interleave(3, "z_bf3", nc.scalar.copy)
-        interleave(2, "own_last1", nc.vector.tensor_copy)
-        second_product(1, nc.vector.tensor_copy)
-        second_product(0, nc.vector.tensor_copy)
-        second_product(2, nc.scalar.copy)
-        second_product(3, nc.scalar.copy)
+        mix(0)
+        mix(1)
+        second_product(0)
+        mix(2)
+        second_product(1)
+        mix(3)
+        second_product(2)
+        second_product(3)

@@ -26,6 +26,7 @@ def tile_picked_mixup_none_p_kernel(tc, x_words, x_scales, w1, w2, lam, mu, offs
     nc = tc.nc
     with ExitStack() as ctx:
         keep = ctx.enter_context(tc.tile_pool(name="keep", bufs=1))
+        loads = ctx.enter_context(tc.tile_pool(name="loads", bufs=1))
         psum = ctx.enter_context(tc.psum_pool(name="psum", bufs=1))
 
         offs_sb = keep.tile([P, S // 16], U16, name="offs_sb")
@@ -36,26 +37,26 @@ def tile_picked_mixup_none_p_kernel(tc, x_words, x_scales, w1, w2, lam, mu, offs
         ident = keep.tile([P, P], F32, name="ident", align_bytes=64)
 
         nc.gpsimd.memset(scales[:].bitcast(I32), 0)
-        zeros = keep.tile([P, P], F32, name="zeros", tag="raw", align_bytes=64)
+        zeros = loads.tile([P, P], F32, name="zeros", offset=4 * (4 * N - P // 2))
         nc.gpsimd.memset(zeros[:], 0.0)
         nc.gpsimd.affine_select(
             out=ident[:], in_=zeros[:], pattern=[[-1, P]], compare_op=mybir.AluOpType.not_equal, fill=1.0, base=0, channel_multiplier=1
         )
-        nc.gpsimd.tensor_scalar(lam_rows[:], ident[:], 1.0, 0.0, MULT, ADD)
+        nc.scalar.copy(lam_rows[:], ident[:])
 
         nc.sync.dma_start(offs_sb[:], offs)
         nc.sync.dma_start(words[:].bitcast(I32), x_words[0].bitcast(I32))
         nc.sync.dma_start(pos_sb[:], pos1)
         for q in range(4):
             nc.sync.dma_start(scales[32 * q : 32 * q + 4, :].bitcast(I32), x_scales[0, 4 * q : 4 * q + 4, :].bitcast(I32))
-        raw = keep.tile([P, 4 * (H + N) + S], F32, name="raw", tag="raw", align_bytes=64)
-        w1_raw = raw[:, 0 : 4 * H].rearrange("p (c j n) -> p c j n", c=2, j=4)
-        w2_raw = raw[:, 4 * H : 4 * (H + N)].rearrange("p (j n) -> p j n", j=4)
-        mu_sb = raw[:, 4 * (H + N) :]
-        w1_rows = w1.rearrange("(p j) c -> p j c", j=4)
-        for c in range(2):
-            nc.sync.dma_start(w1_raw[:, c], w1_rows[:, :, 256 * c : 256 * (c + 1)])
-        nc.sync.dma_start(w2_raw, w2.rearrange("(p j) n -> p j n", j=4))
+        w2_raw = loads.tile([P, 4, N], F32, name="w2_raw", offset=0)
+        raw = loads.tile([P, 4 * H + S], F32, name="raw", offset=4 * 4 * N)
+        w1_raw = raw[:, 0 : 4 * H].rearrange("p (j c) -> p j c", j=4)
+        mu_sb = raw[:, 4 * H :]
+        nc.sync.dma_start(raw[:, 0 : 4 * H], w1.rearrange("(p j) c -> p (j c)", j=4))
+        w2_rows = w2.rearrange("(a t e) n -> e a t n", t=4, e=2)
+        for e in range(2):
+            nc.sync.dma_start(w2_raw[e:P:2], w2_rows[e])
         nc.sync.dma_start(mu_sb, mu)
         nc.sync.dma_start(lam_rows[0:NB, :], lam[0].rearrange("(b p) -> b p", p=P))
 
@@ -70,10 +71,9 @@ def tile_picked_mixup_none_p_kernel(tc, x_words, x_scales, w1, w2, lam, mu, offs
         h_sb = [keep.tile([P, S], F32, name="h_sb%d" % t, align_bytes=64) for t in range(4)]
         partner = keep.tile([P, 4, S], F32, name="partner", align_bytes=64)
 
-        def cast_w1(c, u, copy):
-            src = w1_raw[:, c].rearrange("p j (m u e) -> p u m j e", u=2, e=2)[:, u]
-            dst = w1_bf[u][:].rearrange("p e (c m j) -> p c m j e", c=2, j=4)[:, c]
-            copy(dst, src)
+        def cast_w1(t, copy):
+            src = w1_raw.rearrange("p j (a t e) -> p t a j e", t=4, e=2)[:, t]
+            copy(w1_bf[t // 2][:, t % 2, :].rearrange("p (a e j) -> p a j e", e=2, j=4), src)
 
         def quantize_w1(first, last):
             cols = slice(P * first, P * last)
@@ -95,10 +95,10 @@ def tile_picked_mixup_none_p_kernel(tc, x_words, x_scales, w1, w2, lam, mu, offs
             )
             copy(h_sb[t][:, cols], bank[:])
 
-        cast_w1(0, 0, nc.scalar.copy)
-        cast_w1(0, 1, nc.scalar.copy)
-        cast_w1(1, 0, nc.vector.tensor_copy)
-        cast_w1(1, 1, nc.scalar.copy)
+        cast_w1(0, nc.vector.tensor_copy)
+        cast_w1(1, nc.vector.tensor_copy)
+        cast_w1(2, nc.scalar.copy)
+        cast_w1(3, nc.scalar.copy)
         quantize_w1(0, 1)
         quantize_w1(1, 2)
         quantize_w1(2, 4)
@@ -111,7 +111,7 @@ def tile_picked_mixup_none_p_kernel(tc, x_words, x_scales, w1, w2, lam, mu, offs
         w2_scale = keep.tile([P, N], U8, name="w2_scale", align_bytes=64)
         nc.vector.tensor_copy(
             w2_bf[:].rearrange("p (a e j) -> p a j e", e=4, j=4),
-            w2_raw.rearrange("p j (a e) -> p a j e", e=4),
+            w2_raw[:].rearrange("p j (a e) -> p a j e", e=4),
         )
 
         nc.vector.quantize_mx(out=w2_codes[:].bitcast(FP8X4), scales=w2_scale[:], in_=w2_bf[:])
@@ -140,7 +140,8 @@ def tile_picked_mixup_none_p_kernel(tc, x_words, x_scales, w1, w2, lam, mu, offs
                 )
 
         z_bf = [keep.tile([P, 4 * P], BF16, name="z_bf%d" % b, align_bytes=64) for b in range(NB)]
-        z_codes = [keep.tile([P, P], U32, name="z_codes%d" % b, align_bytes=64) for b in range(NB)]
+        z_words = keep.tile([P, S], U32, name="z_words", tag="own_t3", align_bytes=64)
+        z_codes = [z_words[:, P * b : P * (b + 1)] for b in range(NB)]
         z_scale = [keep.tile([P, P], U8, name="z_scale%d" % b, align_bytes=64) for b in range(NB)]
         res = [keep.tile([P, P], F32, name="res%d" % b, align_bytes=64) for b in range(NB)]
 
@@ -153,13 +154,13 @@ def tile_picked_mixup_none_p_kernel(tc, x_words, x_scales, w1, w2, lam, mu, offs
             )
 
         def second_product(b):
-            nc.vector.quantize_mx(out=z_codes[b][:].bitcast(FP8X4), scales=z_scale[b][:], in_=z_bf[b][:])
+            nc.vector.quantize_mx(out=z_codes[b].bitcast(FP8X4), scales=z_scale[b][:], in_=z_bf[b][:])
             out_ps = psum.tile([P, P], F32, name="out_ps%d" % b, tag="t%d" % b)
             nc.tensor.matmul_mx(
                 out=out_ps[:],
                 lhsT=w2_codes[:].bitcast(FP8X4),
                 lhsT_scale=w2_scale[:],
-                rhs=z_codes[b][:].bitcast(FP8X4),
+                rhs=z_codes[b].bitcast(FP8X4),
                 rhs_scale=z_scale[b][:],
                 start=True,
                 stop=True,

@@ -44,8 +44,8 @@ def tile_picked_mixup_none_p_kernel(tc, x_words, x_scales, w1, w2, lam, mu, offs
         )
         nc.scalar.copy(lam_rows[:], ident[:])
 
-        nc.sync.dma_start(offs_sb[:], offs)
         nc.sync.dma_start(words[:].bitcast(I32), x_words[0].bitcast(I32))
+        nc.sync.dma_start(offs_sb[:], offs)
         nc.sync.dma_start(pos_sb[:], pos1)
         for q in range(4):
             nc.sync.dma_start(scales[32 * q : 32 * q + 4, :].bitcast(I32), x_scales[0, 4 * q : 4 * q + 4, :].bitcast(I32))
@@ -65,20 +65,19 @@ def tile_picked_mixup_none_p_kernel(tc, x_words, x_scales, w1, w2, lam, mu, offs
         nc.vector.tensor_copy(x_codes[:], words[:].indirect(offs_sb[:]))
         nc.vector.tensor_copy(x_scale[:], scales[:].indirect(offs_sb[:]))
 
-        w1_bf = [keep.tile([P, 2, P * 4], BF16, name="w1_bf%d" % u, align_bytes=64) for u in range(2)]
+        first_bf = keep.tile([P, 4 * P], BF16, name="first_bf", tag="staged", align_bytes=64)
+        third_bf = keep.tile([P, 4 * P], BF16, name="third_bf", align_bytes=64)
         w1_codes = keep.tile([P, 4 * P], U32, name="w1_codes", align_bytes=64)
         w1_scale = keep.tile([P, 4 * P], U8, name="w1_scale", align_bytes=64)
         h_sb = [keep.tile([P, S], F32, name="h_sb%d" % t, align_bytes=64) for t in range(4)]
         partner = keep.tile([P, 4, S], F32, name="partner", align_bytes=64)
 
-        def cast_w1(t, copy):
-            src = w1_raw.rearrange("p j (a t e) -> p t a j e", t=4, e=2)[:, t]
-            copy(w1_bf[t // 2][:, t % 2, :].rearrange("p (a e j) -> p a j e", e=2, j=4), src)
+        def cast_w1(t, staged, pairs, copy):
+            src = w1_raw.rearrange("p j (a t e) -> p t a j e", t=4, e=2)[:, t, pairs]
+            copy(staged.rearrange("p (a e j) -> p a j e", e=2, j=4)[:, pairs], src)
 
-        def quantize_w1(first, last):
-            cols = slice(P * first, P * last)
-            u = first // 2
-            staged = w1_bf[u][:, first - 2 * u : last - 2 * u, :].rearrange("p e w -> p (e w)")
+        def quantize_w1(t, staged):
+            cols = slice(P * t, P * (t + 1))
             nc.vector.quantize_mx(out=w1_codes[:, cols].bitcast(FP8X4), scales=w1_scale[:, cols], in_=staged)
 
         def first_product(t, half, copy):
@@ -95,26 +94,28 @@ def tile_picked_mixup_none_p_kernel(tc, x_words, x_scales, w1, w2, lam, mu, offs
             )
             copy(h_sb[t][:, cols], bank[:])
 
-        cast_w1(0, nc.vector.tensor_copy)
-        cast_w1(1, nc.vector.tensor_copy)
-        cast_w1(2, nc.scalar.copy)
-        cast_w1(3, nc.scalar.copy)
-        quantize_w1(0, 1)
-        quantize_w1(1, 2)
-        quantize_w1(2, 4)
-        for t in range(4):
-            first_product(t, 0, nc.scalar.copy)
-            first_product(t, 1, nc.scalar.copy)
-
-        w2_bf = keep.tile([P, 4 * N], BF16, name="w2_bf", tag="w1_bf1", align_bytes=64)
+        cast_w1(0, first_bf[:], slice(0, 40), nc.vector.tensor_copy)
+        cast_w1(0, first_bf[:], slice(40, 64), nc.scalar.copy)
+        quantize_w1(0, first_bf[:])
+        odd_bf = keep.tile([P, 2, 4 * P], BF16, name="odd_bf", tag="staged", align_bytes=64)
+        cast_w1(2, third_bf[:], slice(0, 64), nc.scalar.copy)
+        cast_w1(1, odd_bf[:, 0, :], slice(0, 64), nc.vector.tensor_copy)
+        cast_w1(3, odd_bf[:, 1, :], slice(0, 40), nc.scalar.copy)
+        cast_w1(3, odd_bf[:, 1, :], slice(40, 64), nc.vector.tensor_copy)
+        quantize_w1(1, odd_bf[:, 0, :])
+        quantize_w1(2, third_bf[:])
+        w2_bf = keep.tile([P, 4 * N], BF16, name="w2_bf", tag="third_bf", align_bytes=64)
         w2_codes = keep.tile([P, N], U32, name="w2_codes", align_bytes=64)
         w2_scale = keep.tile([P, N], U8, name="w2_scale", align_bytes=64)
         nc.vector.tensor_copy(
             w2_bf[:].rearrange("p (a e j) -> p a j e", e=4, j=4),
             w2_raw[:].rearrange("p j (a e) -> p a j e", e=4),
         )
-
+        quantize_w1(3, odd_bf[:, 1, :])
         nc.vector.quantize_mx(out=w2_codes[:].bitcast(FP8X4), scales=w2_scale[:], in_=w2_bf[:])
+        for t in range(4):
+            first_product(t, 0, nc.scalar.copy)
+            first_product(t, 1, nc.scalar.copy)
 
         lam_ps = psum.tile([P, P], F32, name="lam_ps", tag="a0")
         lam_cols = keep.tile([P, NB], F32, name="lam_cols")
@@ -153,7 +154,7 @@ def tile_picked_mixup_none_p_kernel(tc, x_words, x_scales, w1, w2, lam, mu, offs
                 ADD,
             )
 
-        def second_product(b):
+        def second_product(b, copy):
             nc.vector.quantize_mx(out=z_codes[b].bitcast(FP8X4), scales=z_scale[b][:], in_=z_bf[b][:])
             out_ps = psum.tile([P, P], F32, name="out_ps%d" % b, tag="t%d" % b)
             nc.tensor.matmul_mx(
@@ -165,14 +166,14 @@ def tile_picked_mixup_none_p_kernel(tc, x_words, x_scales, w1, w2, lam, mu, offs
                 start=True,
                 stop=True,
             )
-            nc.scalar.copy(res[b][:], out_ps[:])
+            copy(res[b][:], out_ps[:])
             nc.sync.dma_start(out[:, P * b : P * (b + 1)], res[b][:])
 
         mix(0)
         mix(1)
-        second_product(0)
+        second_product(0, nc.scalar.copy)
         mix(2)
-        second_product(1)
+        second_product(1, nc.scalar.copy)
         mix(3)
-        second_product(2)
-        second_product(3)
+        second_product(2, nc.scalar.copy)
+        second_product(3, nc.vector.tensor_copy)

@@ -47,8 +47,8 @@ def tile_picked_mixup_none_p_kernel(tc, x_words, x_scales, w1, w2, lam, mu, offs
         nc.sync.dma_start(words[:].bitcast(I32), x_words[0].bitcast(I32))
         nc.sync.dma_start(offs_sb[:], offs)
         nc.sync.dma_start(pos_sb[:], pos1)
-        for q in range(4):
-            nc.sync.dma_start(scales[32 * q : 32 * q + 4, :].bitcast(I32), x_scales[0, 4 * q : 4 * q + 4, :].bitcast(I32))
+        for r in range(4):
+            nc.sync.dma_start(scales[r:P:32, :].bitcast(I32), x_scales[0, r:16:4, :].bitcast(I32))
         w2_raw = loads.tile([P, 4, N], F32, name="w2_raw", offset=0)
         raw = loads.tile([P, 4 * H + S], F32, name="raw", offset=4 * 4 * N)
         w1_raw = raw[:, 0 : 4 * H].rearrange("p (j c) -> p j c", j=4)
@@ -141,7 +141,7 @@ def tile_picked_mixup_none_p_kernel(tc, x_words, x_scales, w1, w2, lam, mu, offs
                 )
 
         z_bf = [keep.tile([P, 4 * P], BF16, name="z_bf%d" % b, align_bytes=64) for b in range(NB)]
-        z_words = keep.tile([P, S], U32, name="z_words", tag="own_t3", align_bytes=64)
+        z_words = keep.tile([P, S], U32, name="z_words", align_bytes=64)
         z_codes = [z_words[:, P * b : P * (b + 1)] for b in range(NB)]
         z_scale = [keep.tile([P, P], U8, name="z_scale%d" % b, align_bytes=64) for b in range(NB)]
         res = [keep.tile([P, P], F32, name="res%d" % b, align_bytes=64) for b in range(NB)]
@@ -156,7 +156,7 @@ def tile_picked_mixup_none_p_kernel(tc, x_words, x_scales, w1, w2, lam, mu, offs
 
         def second_product(b, copy):
             nc.vector.quantize_mx(out=z_codes[b].bitcast(FP8X4), scales=z_scale[b][:], in_=z_bf[b][:])
-            out_ps = psum.tile([P, P], F32, name="out_ps%d" % b, tag="t%d" % b)
+            out_ps = psum.tile([P, P], F32, name="out_ps%d" % b, tag="t%d" % (NB - 1 - b))
             nc.tensor.matmul_mx(
                 out=out_ps[:],
                 lhsT=w2_codes[:].bitcast(FP8X4),

@@ -20,6 +20,7 @@ COPY = mybir.ActivationFunctionType.Copy
 P = 128
 NB = S // P
 HALF = S // 2
+SPARE = 16
 
 
 def tile_picked_mixup_none_p_kernel(tc, x_words, x_scales, w1, w2, lam, mu, offs, pos1, out):
@@ -36,7 +37,7 @@ def tile_picked_mixup_none_p_kernel(tc, x_words, x_scales, w1, w2, lam, mu, offs
         lam_rows = keep.tile([P, P], F32, name="lam_rows", align_bytes=64)
         ident = keep.tile([P, P], F32, name="ident", align_bytes=64)
 
-        nc.gpsimd.memset(scales[:].bitcast(I32), 0)
+        nc.vector.memset(scales[:].bitcast(I32), 0)
         zeros = loads.tile([P, P], F32, name="zeros", offset=4 * (4 * N - P // 2))
         nc.gpsimd.memset(zeros[:], 0.0)
         nc.gpsimd.affine_select(
@@ -69,7 +70,9 @@ def tile_picked_mixup_none_p_kernel(tc, x_words, x_scales, w1, w2, lam, mu, offs
         third_bf = keep.tile([P, 4 * P], BF16, name="third_bf", align_bytes=64)
         w1_codes = keep.tile([P, 4 * P], U32, name="w1_codes", align_bytes=64)
         w1_scale = keep.tile([P, 4 * P], U8, name="w1_scale", align_bytes=64)
-        h_sb = [keep.tile([P, S], F32, name="h_sb%d" % t, align_bytes=64) for t in range(4)]
+        h_sb = [keep.tile([P, S + SPARE if t < 3 else S], F32, name="h_sb%d" % t, align_bytes=64) for t in range(4)]
+        for t in range(3):
+            nc.vector.memset(h_sb[t][:, S:], 0.0)
         partner = keep.tile([P, 4, S], F32, name="partner", align_bytes=64)
 
         def cast_w1(t, staged, pairs, copy):
@@ -133,12 +136,11 @@ def tile_picked_mixup_none_p_kernel(tc, x_words, x_scales, w1, w2, lam, mu, offs
             for t in range(4):
                 nc.tensor.transpose(own_ps[b][:, t, :], own_t[b][:, t, :], ident[:])
 
-        for t in range(4):
-            for half in range(2):
-                cols = slice(HALF * half, HALF * (half + 1))
-                nc.vector.tensor_tensor(
-                    partner[:, t, cols], h_sb[t][:].indirect(pos_sb[:, 16 * half : 16 * (half + 1)]), mu_sb[:, cols], MULT
-                )
+        for t in range(3):
+            nc.vector.tensor_tensor(partner[:, t, :], h_sb[t][:].indirect(pos_sb[:]), mu_sb, MULT)
+        for half in range(2):
+            cols = slice(HALF * half, HALF * (half + 1))
+            nc.vector.tensor_tensor(partner[:, 3, cols], h_sb[3][:].indirect(pos_sb[:, 16 * half : 16 * (half + 1)]), mu_sb[:, cols], MULT)
 
         z_bf = [keep.tile([P, 4 * P], BF16, name="z_bf%d" % b, align_bytes=64) for b in range(NB)]
         z_words = keep.tile([P, S], U32, name="z_words", align_bytes=64)

@@ -38,23 +38,25 @@ def tile_picked_mixup_none_p_kernel(tc, x_words, x_scales, w1, w2, lam, mu, offs
         ident = keep.tile([P, P], F32, name="ident", align_bytes=64)
 
         nc.vector.memset(scales[:].bitcast(I32), 0)
-        zeros = loads.tile([P, P], F32, name="zeros", offset=4 * (4 * N - P // 2))
-        nc.gpsimd.memset(zeros[:], 0.0)
+        zeros = keep.tile([P, P], F32, name="zeros")
+        nc.vector.memset(zeros[:], 0.0)
         nc.gpsimd.affine_select(
             out=ident[:], in_=zeros[:], pattern=[[-1, P]], compare_op=mybir.AluOpType.not_equal, fill=1.0, base=0, channel_multiplier=1
         )
-        nc.scalar.copy(lam_rows[:], ident[:])
+        nc.scalar.copy(lam_rows[:], zeros[:])
 
         nc.sync.dma_start(words[:].bitcast(I32), x_words[0].bitcast(I32))
         nc.sync.dma_start(offs_sb[:], offs)
-        nc.sync.dma_start(pos_sb[:], pos1)
         for r in range(4):
             nc.sync.dma_start(scales[r:P:32, :].bitcast(I32), x_scales[0, r:16:4, :].bitcast(I32))
         w2_raw = loads.tile([P, 4, N], F32, name="w2_raw", offset=0)
         raw = loads.tile([P, 4 * H + S], F32, name="raw", offset=4 * 4 * N)
         w1_raw = raw[:, 0 : 4 * H].rearrange("p (j c) -> p j c", j=4)
         mu_sb = raw[:, 4 * H :]
-        nc.sync.dma_start(raw[:, 0 : 4 * H], w1.rearrange("(p j) c -> p (j c)", j=4))
+        w1_rows = w1.rearrange("(p j) c -> p (j c)", j=4)
+        for part in range(2):
+            nc.sync.dma_start(raw[:, 2 * H * part : 2 * H * (part + 1)], w1_rows[:, 2 * H * part : 2 * H * (part + 1)])
+        nc.sync.dma_start(pos_sb[:], pos1)
         w2_rows = w2.rearrange("(a t e) n -> e a t n", t=4, e=2)
         for e in range(2):
             nc.sync.dma_start(w2_raw[e:P:2], w2_rows[e])
@@ -66,8 +68,7 @@ def tile_picked_mixup_none_p_kernel(tc, x_words, x_scales, w1, w2, lam, mu, offs
         nc.vector.tensor_copy(x_codes[:], words[:].indirect(offs_sb[:]))
         nc.vector.tensor_copy(x_scale[:], scales[:].indirect(offs_sb[:]))
 
-        first_bf = keep.tile([P, 4 * P], BF16, name="first_bf", tag="staged", align_bytes=64)
-        third_bf = keep.tile([P, 4 * P], BF16, name="third_bf", align_bytes=64)
+        w1_bf = [keep.tile([P, 4 * P], BF16, name="w1_bf%d" % t, tag="w1_bf%d" % t, align_bytes=64) for t in range(4)]
         w1_codes = keep.tile([P, 4 * P], U32, name="w1_codes", align_bytes=64)
         w1_scale = keep.tile([P, 4 * P], U8, name="w1_scale", align_bytes=64)
         h_sb = [keep.tile([P, S + SPARE if t < 3 else S], F32, name="h_sb%d" % t, align_bytes=64) for t in range(4)]
@@ -75,9 +76,9 @@ def tile_picked_mixup_none_p_kernel(tc, x_words, x_scales, w1, w2, lam, mu, offs
             nc.vector.memset(h_sb[t][:, S:], 0.0)
         partner = keep.tile([P, 4, S], F32, name="partner", align_bytes=64)
 
-        def cast_w1(t, staged, pairs, copy):
-            src = w1_raw.rearrange("p j (a t e) -> p t a j e", t=4, e=2)[:, t, pairs]
-            copy(staged.rearrange("p (a e j) -> p a j e", e=2, j=4)[:, pairs], src)
+        def cast_w1(t, rows, copy):
+            src = w1_raw.rearrange("p j (a t e) -> p t a j e", t=4, e=2)[:, t, :, rows]
+            copy(w1_bf[t][:].rearrange("p (a e j) -> p a j e", e=2, j=4)[:, :, rows], src)
 
         def quantize_w1(t, staged):
             cols = slice(P * t, P * (t + 1))
@@ -97,24 +98,23 @@ def tile_picked_mixup_none_p_kernel(tc, x_words, x_scales, w1, w2, lam, mu, offs
             )
             copy(h_sb[t][:, cols], bank[:])
 
-        cast_w1(0, first_bf[:], slice(0, 40), nc.vector.tensor_copy)
-        cast_w1(0, first_bf[:], slice(40, 64), nc.scalar.copy)
-        quantize_w1(0, first_bf[:])
-        odd_bf = keep.tile([P, 2, 4 * P], BF16, name="odd_bf", tag="staged", align_bytes=64)
-        cast_w1(2, third_bf[:], slice(0, 64), nc.scalar.copy)
-        cast_w1(1, odd_bf[:, 0, :], slice(0, 64), nc.vector.tensor_copy)
-        cast_w1(3, odd_bf[:, 1, :], slice(0, 40), nc.scalar.copy)
-        cast_w1(3, odd_bf[:, 1, :], slice(40, 64), nc.vector.tensor_copy)
-        quantize_w1(1, odd_bf[:, 0, :])
-        quantize_w1(2, third_bf[:])
-        w2_bf = keep.tile([P, 4 * N], BF16, name="w2_bf", tag="third_bf", align_bytes=64)
+        for t in range(3):
+            cast_w1(t, slice(0, 2), nc.scalar.copy)
+        cast_w1(0, slice(2, 4), nc.vector.tensor_copy)
+        quantize_w1(0, w1_bf[0][:])
+        cast_w1(1, slice(2, 4), nc.vector.tensor_copy)
+        cast_w1(2, slice(2, 4), nc.scalar.copy)
+        cast_w1(3, slice(0, 4), nc.scalar.copy)
+        quantize_w1(1, w1_bf[1][:])
+        quantize_w1(2, w1_bf[2][:])
+        w2_bf = keep.tile([P, 4 * N], BF16, name="w2_bf", tag="w1_bf1", align_bytes=64)
         w2_codes = keep.tile([P, N], U32, name="w2_codes", align_bytes=64)
         w2_scale = keep.tile([P, N], U8, name="w2_scale", align_bytes=64)
         nc.vector.tensor_copy(
             w2_bf[:].rearrange("p (a e j) -> p a j e", e=4, j=4),
             w2_raw[:].rearrange("p j (a e) -> p a j e", e=4),
         )
-        quantize_w1(3, odd_bf[:, 1, :])
+        quantize_w1(3, w1_bf[3][:])
         nc.vector.quantize_mx(out=w2_codes[:].bitcast(FP8X4), scales=w2_scale[:], in_=w2_bf[:])
         for t in range(4):
             first_product(t, 0, nc.scalar.copy)
@@ -146,7 +146,8 @@ def tile_picked_mixup_none_p_kernel(tc, x_words, x_scales, w1, w2, lam, mu, offs
         z_words = keep.tile([P, S], U32, name="z_words", align_bytes=64)
         z_codes = [z_words[:, P * b : P * (b + 1)] for b in range(NB)]
         z_scale = [keep.tile([P, P], U8, name="z_scale%d" % b, align_bytes=64) for b in range(NB)]
-        res = [keep.tile([P, P], F32, name="res%d" % b, align_bytes=64) for b in range(NB)]
+        res_pair = keep.tile([P, 2 * P], F32, name="res_pair", align_bytes=64)
+        res = [res_pair[:, 0:P], res_pair[:, P:]] + [keep.tile([P, P], F32, name="res%d" % b, align_bytes=64)[:] for b in (2, 3)]
 
         def mix(b):
             nc.vector.tensor_tensor(
@@ -168,8 +169,11 @@ def tile_picked_mixup_none_p_kernel(tc, x_words, x_scales, w1, w2, lam, mu, offs
                 start=True,
                 stop=True,
             )
-            copy(res[b][:], out_ps[:])
-            nc.sync.dma_start(out[:, P * b : P * (b + 1)], res[b][:])
+            copy(res[b], out_ps[:])
+            if b == 1:
+                nc.sync.dma_start(out[:, 0 : 2 * P], res_pair[:])
+            elif b > 1:
+                nc.sync.dma_start(out[:, P * b : P * (b + 1)], res[b])
 
         mix(0)
         mix(1)

@@ -21,6 +21,7 @@ P = 128
 NB = S // P
 HALF = S // 2
 SPARE = 16
+SIDE = 64
 
 
 def tile_picked_mixup_none_p_kernel(tc, x_words, x_scales, w1, w2, lam, mu, offs, pos1, out):
@@ -84,9 +85,8 @@ def tile_picked_mixup_none_p_kernel(tc, x_words, x_scales, w1, w2, lam, mu, offs
             cols = slice(P * t, P * (t + 1))
             nc.vector.quantize_mx(out=w1_codes[:, cols].bitcast(FP8X4), scales=w1_scale[:, cols], in_=staged)
 
-        def first_product(t, half, copy):
-            cols = slice(HALF * half, HALF * (half + 1))
-            bank = psum.tile([P, HALF], F32, name="h_ps%d_%d" % (t, half), tag="a%d" % (2 * (t % 2) + half))
+        def first_product(t, cols, tag):
+            bank = psum.tile([P, cols.stop - cols.start], F32, name="h_ps%d_%d" % (t, cols.start), tag=tag)
             nc.tensor.matmul_mx(
                 out=bank[:],
                 lhsT=w1_codes[:, P * t : P * (t + 1)].bitcast(FP8X4),
@@ -96,7 +96,7 @@ def tile_picked_mixup_none_p_kernel(tc, x_words, x_scales, w1, w2, lam, mu, offs
                 start=True,
                 stop=True,
             )
-            copy(h_sb[t][:, cols], bank[:])
+            nc.scalar.copy(h_sb[t][:, cols], bank[:])
 
         for t in range(3):
             cast_w1(t, slice(0, 2), nc.scalar.copy)
@@ -116,11 +116,12 @@ def tile_picked_mixup_none_p_kernel(tc, x_words, x_scales, w1, w2, lam, mu, offs
         )
         quantize_w1(3, w1_bf[3][:])
         nc.vector.quantize_mx(out=w2_codes[:].bitcast(FP8X4), scales=w2_scale[:], in_=w2_bf[:])
-        for t in range(4):
-            first_product(t, 0, nc.scalar.copy)
-            first_product(t, 1, nc.scalar.copy)
+        first_product(0, slice(0, HALF), "a0")
+        first_product(0, slice(HALF, S), "a1")
+        for t in range(1, 4):
+            first_product(t, slice(0, S), "a%d" % ((t + 1) % 4))
 
-        lam_ps = psum.tile([P, P], F32, name="lam_ps", tag="a0")
+        lam_ps = psum.tile([P, P], F32, name="lam_ps", tag="a1")
         lam_cols = keep.tile([P, NB], F32, name="lam_cols")
         nc.tensor.transpose(lam_ps[:], lam_rows[:], ident[:])
         nc.scalar.copy(lam_cols[:], lam_ps[:, 0:NB])
@@ -130,11 +131,14 @@ def tile_picked_mixup_none_p_kernel(tc, x_words, x_scales, w1, w2, lam, mu, offs
             for b in range(NB):
                 nc.tensor.transpose(ht_ps[b][:, t, :], h_sb[t][:, P * b : P * (b + 1)], ident[:])
         own_t = [keep.tile([P, 4, P], F32, name="own_t%d" % b, align_bytes=64) for b in range(NB)]
+        own_first = keep.tile([P, 4, SIDE], F32, name="own_first", tag="z_words", align_bytes=64)
         own_ps = [psum.tile([P, 4, P], F32, name="own_ps%d" % b, tag="a%d" % b) for b in range(NB)]
         for b in range(NB):
             nc.scalar.activation(own_t[b][:], ht_ps[b][:], COPY, scale=lam_cols[:, b : b + 1])
             for t in range(4):
                 nc.tensor.transpose(own_ps[b][:, t, :], own_t[b][:, t, :], ident[:])
+            if b == 1:
+                nc.scalar.copy(own_first[:], own_ps[0][:, :, 0:SIDE])
 
         for t in range(3):
             nc.vector.tensor_tensor(partner[:, t, :], h_sb[t][:].indirect(pos_sb[:]), mu_sb, MULT)
@@ -142,44 +146,45 @@ def tile_picked_mixup_none_p_kernel(tc, x_words, x_scales, w1, w2, lam, mu, offs
             cols = slice(HALF * half, HALF * (half + 1))
             nc.vector.tensor_tensor(partner[:, 3, cols], h_sb[3][:].indirect(pos_sb[:, 16 * half : 16 * (half + 1)]), mu_sb[:, cols], MULT)
 
-        z_bf = [keep.tile([P, 4 * P], BF16, name="z_bf%d" % b, align_bytes=64) for b in range(NB)]
-        z_words = keep.tile([P, S], U32, name="z_words", align_bytes=64)
-        z_codes = [z_words[:, P * b : P * (b + 1)] for b in range(NB)]
-        z_scale = [keep.tile([P, P], U8, name="z_scale%d" % b, align_bytes=64) for b in range(NB)]
-        res_pair = keep.tile([P, 2 * P], F32, name="res_pair", align_bytes=64)
-        res = [res_pair[:, 0:P], res_pair[:, P:]] + [keep.tile([P, P], F32, name="res%d" % b, align_bytes=64)[:] for b in (2, 3)]
+        z_bf = keep.tile([P, 4 * S], BF16, name="z_bf", align_bytes=64)
 
-        def mix(b):
-            nc.vector.tensor_tensor(
-                z_bf[b][:].rearrange("p (q i t) -> p q t i", i=2, t=4),
-                own_ps[b][:].rearrange("p t (q i) -> p q t i", i=2),
-                partner[:, :, P * b : P * (b + 1)].rearrange("p t (q i) -> p q t i", i=2),
+        def mix(cols, add, own):
+            add(
+                z_bf[:, 4 * cols.start : 4 * cols.stop].rearrange("p (q i t) -> p q t i", i=2, t=4),
+                own.rearrange("p t (q i) -> p q t i", i=2),
+                partner[:, :, cols].rearrange("p t (q i) -> p q t i", i=2),
                 ADD,
             )
 
-        def second_product(b, copy):
-            nc.vector.quantize_mx(out=z_codes[b].bitcast(FP8X4), scales=z_scale[b][:], in_=z_bf[b][:])
-            out_ps = psum.tile([P, P], F32, name="out_ps%d" % b, tag="t%d" % (NB - 1 - b))
+        mix(slice(0, SIDE), nc.gpsimd.tensor_tensor, own_first[:])
+        for b in range(1, NB):
+            mix(slice(P * b, P * (b + 1)), nc.vector.tensor_tensor, own_ps[b][:])
+        mix(slice(SIDE, P), nc.vector.tensor_tensor, own_ps[0][:, :, SIDE:])
+
+        z_words = keep.tile([P, S], U32, name="z_words", tag="z_words", align_bytes=64)
+        z_scale = keep.tile([P, S], U8, name="z_scale", align_bytes=64)
+
+        res = keep.tile([P, S], F32, name="res", align_bytes=64)
+
+        def second_product(b, tag, copy):
+            cols = slice(P * b, P * (b + 1))
+            nc.vector.quantize_mx(out=z_words[:, cols].bitcast(FP8X4), scales=z_scale[:, cols], in_=z_bf[:, 4 * cols.start : 4 * cols.stop])
+            out_ps = psum.tile([P, P], F32, name="out_ps%d" % b, tag=tag)
             nc.tensor.matmul_mx(
                 out=out_ps[:],
                 lhsT=w2_codes[:].bitcast(FP8X4),
                 lhsT_scale=w2_scale[:],
-                rhs=z_codes[b].bitcast(FP8X4),
-                rhs_scale=z_scale[b][:],
+                rhs=z_words[:, cols].bitcast(FP8X4),
+                rhs_scale=z_scale[:, cols],
                 start=True,
                 stop=True,
             )
-            copy(res[b], out_ps[:])
-            if b == 1:
-                nc.sync.dma_start(out[:, 0 : 2 * P], res_pair[:])
-            elif b > 1:
-                nc.sync.dma_start(out[:, P * b : P * (b + 1)], res[b])
+            copy(res[:, cols], out_ps[:])
 
-        mix(0)
-        mix(1)
-        second_product(0, nc.scalar.copy)
-        mix(2)
-        second_product(1, nc.scalar.copy)
-        mix(3)
-        second_product(2, nc.scalar.copy)
-        second_product(3, nc.vector.tensor_copy)
+        second_product(1, "t3", nc.scalar.copy)
+        second_product(2, "t2", nc.scalar.copy)
+        nc.sync.dma_start(out[:, P : 3 * P], res[:, P : 3 * P])
+        second_product(3, "t1", nc.scalar.copy)
+        nc.sync.dma_start(out[:, 3 * P :], res[:, 3 * P :])
+        second_product(0, "t0", nc.vector.tensor_copy)
+        nc.sync.dma_start(out[:, 0:P], res[:, 0:P])

@@ -21,7 +21,7 @@ P = 128
 NB = S // P
 HALF = S // 2
 SPARE = 16
-SIDE = 64
+SIDE = 112
 
 
 def tile_picked_mixup_none_p_kernel(tc, x_words, x_scales, w1, w2, lam, mu, offs, pos1, out):
@@ -118,8 +118,9 @@ def tile_picked_mixup_none_p_kernel(tc, x_words, x_scales, w1, w2, lam, mu, offs
         nc.vector.quantize_mx(out=w2_codes[:].bitcast(FP8X4), scales=w2_scale[:], in_=w2_bf[:])
         first_product(0, slice(0, HALF), "a0")
         first_product(0, slice(HALF, S), "a1")
-        for t in range(1, 4):
-            first_product(t, slice(0, S), "a%d" % ((t + 1) % 4))
+        first_product(1, slice(0, S), "a2")
+        for b in range(NB):
+            first_product(2 + b // 2, slice(HALF * (b % 2), HALF * (b % 2 + 1)), "t%d" % b)
 
         lam_ps = psum.tile([P, P], F32, name="lam_ps", tag="a1")
         lam_cols = keep.tile([P, NB], F32, name="lam_cols")
@@ -127,16 +128,16 @@ def tile_picked_mixup_none_p_kernel(tc, x_words, x_scales, w1, w2, lam, mu, offs
         nc.scalar.copy(lam_cols[:], lam_ps[:, 0:NB])
 
         ht_ps = [psum.tile([P, 4, P], F32, name="ht_ps%d" % b, tag="t%d" % b) for b in range(NB)]
-        for t in range(4):
-            for b in range(NB):
+        for b in range(NB):
+            for t in range(4):
                 nc.tensor.transpose(ht_ps[b][:, t, :], h_sb[t][:, P * b : P * (b + 1)], ident[:])
-        own_t = [keep.tile([P, 4, P], F32, name="own_t%d" % b, align_bytes=64) for b in range(NB)]
         own_first = keep.tile([P, 4, SIDE], F32, name="own_first", tag="z_words", align_bytes=64)
         own_ps = [psum.tile([P, 4, P], F32, name="own_ps%d" % b, tag="a%d" % b) for b in range(NB)]
         for b in range(NB):
-            nc.scalar.activation(own_t[b][:], ht_ps[b][:], COPY, scale=lam_cols[:, b : b + 1])
+            own_t = keep.tile([P, 4, P], F32, name="own_t%d" % b, tag="own_t%d" % (b % 3), align_bytes=64)
+            nc.scalar.activation(own_t[:], ht_ps[b][:], COPY, scale=lam_cols[:, b : b + 1])
             for t in range(4):
-                nc.tensor.transpose(own_ps[b][:, t, :], own_t[b][:, t, :], ident[:])
+                nc.tensor.transpose(own_ps[b][:, t, :], own_t[:, t, :], ident[:])
             if b == 1:
                 nc.scalar.copy(own_first[:], own_ps[0][:, :, 0:SIDE])
 
@@ -156,10 +157,15 @@ def tile_picked_mixup_none_p_kernel(tc, x_words, x_scales, w1, w2, lam, mu, offs
                 ADD,
             )
 
-        mix(slice(0, SIDE), nc.gpsimd.tensor_tensor, own_first[:])
-        for b in range(1, NB):
-            mix(slice(P * b, P * (b + 1)), nc.vector.tensor_tensor, own_ps[b][:])
+        z_side = keep.tile([P, 4, SIDE], F32, name="z_side", align_bytes=64)
+        nc.gpsimd.tensor_tensor(z_side[:], own_first[:], partner[:, :, 0:SIDE], ADD)
+        nc.scalar.copy(
+            z_bf[:, 0 : 4 * SIDE].rearrange("p (q i t) -> p q t i", i=2, t=4),
+            z_side[:].rearrange("p t (q i) -> p q t i", i=2),
+        )
         mix(slice(SIDE, P), nc.vector.tensor_tensor, own_ps[0][:, :, SIDE:])
+        for b in (1, 2):
+            mix(slice(P * b, P * (b + 1)), nc.vector.tensor_tensor, own_ps[b][:])
 
         z_words = keep.tile([P, S], U32, name="z_words", tag="z_words", align_bytes=64)
         z_scale = keep.tile([P, S], U8, name="z_scale", align_bytes=64)
@@ -182,9 +188,10 @@ def tile_picked_mixup_none_p_kernel(tc, x_words, x_scales, w1, w2, lam, mu, offs
             copy(res[:, cols], out_ps[:])
 
         second_product(1, "t3", nc.scalar.copy)
-        second_product(2, "t2", nc.scalar.copy)
+        mix(slice(3 * P, S), nc.vector.tensor_tensor, own_ps[3][:])
+        second_product(2, "t1", nc.scalar.copy)
         nc.sync.dma_start(out[:, P : 3 * P], res[:, P : 3 * P])
-        second_product(3, "t1", nc.scalar.copy)
-        nc.sync.dma_start(out[:, 3 * P :], res[:, 3 * P :])
-        second_product(0, "t0", nc.vector.tensor_copy)
+        second_product(0, "t2", nc.scalar.copy)
         nc.sync.dma_start(out[:, 0:P], res[:, 0:P])
+        second_product(3, "t0", nc.vector.tensor_copy)
+        nc.sync.dma_start(out[:, 3 * P :], res[:, 3 * P :])

@@ -21,7 +21,7 @@ P = 128
 NB = S // P
 HALF = S // 2
 SPARE = 16
-SIDE = 112
+SIDE = 120
 
 
 def tile_picked_mixup_none_p_kernel(tc, x_words, x_scales, w1, w2, lam, mu, offs, pos1, out):
@@ -29,13 +29,14 @@ def tile_picked_mixup_none_p_kernel(tc, x_words, x_scales, w1, w2, lam, mu, offs
     with ExitStack() as ctx:
         keep = ctx.enter_context(tc.tile_pool(name="keep", bufs=1))
         loads = ctx.enter_context(tc.tile_pool(name="loads", bufs=1))
+        shared = ctx.enter_context(tc.tile_pool(name="shared", bufs=1))
         psum = ctx.enter_context(tc.psum_pool(name="psum", bufs=1))
 
         offs_sb = keep.tile([P, S // 16], U16, name="offs_sb")
         pos_sb = keep.tile([P, S // 16], U16, name="pos_sb")
         words = keep.tile([P, T], U16, name="words", align_bytes=64)
         scales = keep.tile([P, T], U8, name="scales", align_bytes=64)
-        lam_rows = keep.tile([P, P], F32, name="lam_rows", align_bytes=64)
+        lam_cols = keep.tile([P, NB], F32, name="lam_cols")
         ident = keep.tile([P, P], F32, name="ident", align_bytes=64)
 
         nc.vector.memset(scales[:].bitcast(I32), 0)
@@ -44,7 +45,6 @@ def tile_picked_mixup_none_p_kernel(tc, x_words, x_scales, w1, w2, lam, mu, offs
         nc.gpsimd.affine_select(
             out=ident[:], in_=zeros[:], pattern=[[-1, P]], compare_op=mybir.AluOpType.not_equal, fill=1.0, base=0, channel_multiplier=1
         )
-        nc.scalar.copy(lam_rows[:], zeros[:])
 
         nc.sync.dma_start(words[:].bitcast(I32), x_words[0].bitcast(I32))
         nc.sync.dma_start(offs_sb[:], offs)
@@ -62,7 +62,8 @@ def tile_picked_mixup_none_p_kernel(tc, x_words, x_scales, w1, w2, lam, mu, offs
         for e in range(2):
             nc.sync.dma_start(w2_raw[e:P:2], w2_rows[e])
         nc.sync.dma_start(mu_sb, mu)
-        nc.sync.dma_start(lam_rows[0:NB, :], lam[0].rearrange("(b p) -> b p", p=P))
+        with nc.allow_non_contiguous_dma(reason="one share a partition and block"):
+            nc.sync.dma_start(lam_cols[:], lam[0].rearrange("(b p) -> p b", p=P))
 
         x_codes = keep.tile([P, S], U16, name="x_codes", align_bytes=64)
         x_scale = keep.tile([P, S], U8, name="x_scale", align_bytes=64)
@@ -74,7 +75,7 @@ def tile_picked_mixup_none_p_kernel(tc, x_words, x_scales, w1, w2, lam, mu, offs
         w1_scale = keep.tile([P, 4 * P], U8, name="w1_scale", align_bytes=64)
         h_sb = [keep.tile([P, S + SPARE if t < 3 else S], F32, name="h_sb%d" % t, align_bytes=64) for t in range(4)]
         for t in range(3):
-            nc.vector.memset(h_sb[t][:, S:], 0.0)
+            nc.scalar.copy(h_sb[t][:, S:], zeros[:, 0:SPARE])
         partner = keep.tile([P, 4, S], F32, name="partner", align_bytes=64)
 
         def cast_w1(t, rows, copy):
@@ -122,19 +123,14 @@ def tile_picked_mixup_none_p_kernel(tc, x_words, x_scales, w1, w2, lam, mu, offs
         for b in range(NB):
             first_product(2 + b // 2, slice(HALF * (b % 2), HALF * (b % 2 + 1)), "t%d" % b)
 
-        lam_ps = psum.tile([P, P], F32, name="lam_ps", tag="a1")
-        lam_cols = keep.tile([P, NB], F32, name="lam_cols")
-        nc.tensor.transpose(lam_ps[:], lam_rows[:], ident[:])
-        nc.scalar.copy(lam_cols[:], lam_ps[:, 0:NB])
-
         ht_ps = [psum.tile([P, 4, P], F32, name="ht_ps%d" % b, tag="t%d" % b) for b in range(NB)]
         for b in range(NB):
             for t in range(4):
                 nc.tensor.transpose(ht_ps[b][:, t, :], h_sb[t][:, P * b : P * (b + 1)], ident[:])
-        own_first = keep.tile([P, 4, SIDE], F32, name="own_first", tag="z_words", align_bytes=64)
+        own_first = shared.tile([P, 4, SIDE], F32, name="own_first", align_bytes=64, offset=0)
         own_ps = [psum.tile([P, 4, P], F32, name="own_ps%d" % b, tag="a%d" % b) for b in range(NB)]
         for b in range(NB):
-            own_t = keep.tile([P, 4, P], F32, name="own_t%d" % b, tag="own_t%d" % (b % 3), align_bytes=64)
+            own_t = shared.tile([P, 4, P], F32, name="own_t%d" % b, align_bytes=64, offset=16 * P * (3 - b % 3))
             nc.scalar.activation(own_t[:], ht_ps[b][:], COPY, scale=lam_cols[:, b : b + 1])
             for t in range(4):
                 nc.tensor.transpose(own_ps[b][:, t, :], own_t[:, t, :], ident[:])
@@ -167,7 +163,7 @@ def tile_picked_mixup_none_p_kernel(tc, x_words, x_scales, w1, w2, lam, mu, offs
         for b in (1, 2):
             mix(slice(P * b, P * (b + 1)), nc.vector.tensor_tensor, own_ps[b][:])
 
-        z_words = keep.tile([P, S], U32, name="z_words", tag="z_words", align_bytes=64)
+        z_words = shared.tile([P, S], U32, name="z_words", align_bytes=64, offset=8 * P)
         z_scale = keep.tile([P, S], U8, name="z_scale", align_bytes=64)
 
         res = keep.tile([P, S], F32, name="res", align_bytes=64)
@@ -188,9 +184,9 @@ def tile_picked_mixup_none_p_kernel(tc, x_words, x_scales, w1, w2, lam, mu, offs
             copy(res[:, cols], out_ps[:])
 
         second_product(1, "t3", nc.scalar.copy)
-        mix(slice(3 * P, S), nc.vector.tensor_tensor, own_ps[3][:])
         second_product(2, "t1", nc.scalar.copy)
         nc.sync.dma_start(out[:, P : 3 * P], res[:, P : 3 * P])
+        mix(slice(3 * P, S), nc.vector.tensor_tensor, own_ps[3][:])
         second_product(0, "t2", nc.scalar.copy)
         nc.sync.dma_start(out[:, 0:P], res[:, 0:P])
         second_product(3, "t0", nc.vector.tensor_copy)

@@ -21,7 +21,6 @@ P = 128
 NB = S // P
 HALF = S // 2
 SPARE = 16
-SIDE = 120
 
 
 def tile_picked_mixup_none_p_kernel(tc, x_words, x_scales, w1, w2, lam, mu, offs, pos1, out):
@@ -127,7 +126,7 @@ def tile_picked_mixup_none_p_kernel(tc, x_words, x_scales, w1, w2, lam, mu, offs
         for b in range(NB):
             for t in range(4):
                 nc.tensor.transpose(ht_ps[b][:, t, :], h_sb[t][:, P * b : P * (b + 1)], ident[:])
-        own_first = shared.tile([P, 4, SIDE], F32, name="own_first", align_bytes=64, offset=0)
+        own_first = shared.tile([P, 4, P], F32, name="own_first", align_bytes=64, offset=0)
         own_ps = [psum.tile([P, 4, P], F32, name="own_ps%d" % b, tag="a%d" % b) for b in range(NB)]
         for b in range(NB):
             own_t = shared.tile([P, 4, P], F32, name="own_t%d" % b, align_bytes=64, offset=16 * P * (3 - b % 3))
@@ -135,7 +134,7 @@ def tile_picked_mixup_none_p_kernel(tc, x_words, x_scales, w1, w2, lam, mu, offs
             for t in range(4):
                 nc.tensor.transpose(own_ps[b][:, t, :], own_t[:, t, :], ident[:])
             if b == 1:
-                nc.scalar.copy(own_first[:], own_ps[0][:, :, 0:SIDE])
+                nc.scalar.copy(own_first[:], own_ps[0][:])
 
         for t in range(3):
             nc.vector.tensor_tensor(partner[:, t, :], h_sb[t][:].indirect(pos_sb[:]), mu_sb, MULT)
@@ -153,13 +152,12 @@ def tile_picked_mixup_none_p_kernel(tc, x_words, x_scales, w1, w2, lam, mu, offs
                 ADD,
             )
 
-        z_side = keep.tile([P, 4, SIDE], F32, name="z_side", align_bytes=64)
-        nc.gpsimd.tensor_tensor(z_side[:], own_first[:], partner[:, :, 0:SIDE], ADD)
+        z_side = keep.tile([P, 4, P], F32, name="z_side", align_bytes=64)
+        nc.gpsimd.tensor_tensor(z_side[:], own_first[:], partner[:, :, 0:P], ADD)
         nc.scalar.copy(
-            z_bf[:, 0 : 4 * SIDE].rearrange("p (q i t) -> p q t i", i=2, t=4),
+            z_bf[:, 0 : 4 * P].rearrange("p (q i t) -> p q t i", i=2, t=4),
             z_side[:].rearrange("p t (q i) -> p q t i", i=2),
         )
-        mix(slice(SIDE, P), nc.vector.tensor_tensor, own_ps[0][:, :, SIDE:])
         for b in (1, 2):
             mix(slice(P * b, P * (b + 1)), nc.vector.tensor_tensor, own_ps[b][:])
 

from contextlib import ExitStack

import concourse.mybir as mybir

K, T, S, H, N = 512, 2048, 512, 512, 128
FLOPS = 2 * K * H * S + 2 * H * N * S

F32 = mybir.dt.float32
BF16 = mybir.dt.bfloat16
I32 = mybir.dt.int32
U32 = mybir.dt.uint32
U16 = mybir.dt.uint16
U8 = mybir.dt.uint8
FP8X4 = mybir.dt.float8_e4m3fn_x4
FP4X4 = mybir.dt.float4_e2m1fn_x4
MULT = mybir.AluOpType.mult
ADD = mybir.AluOpType.add
COPY = mybir.ActivationFunctionType.Copy

P = 128
NB = S // P
HALF = S // 2
SPARE = 16


def tile_picked_mixup_none_p_kernel(tc, x_words, x_scales, w1, w2, lam, mu, offs, pos1, out):
    nc = tc.nc
    with ExitStack() as ctx:
        keep = ctx.enter_context(tc.tile_pool(name="keep", bufs=1))
        loads = ctx.enter_context(tc.tile_pool(name="loads", bufs=1))
        shared = ctx.enter_context(tc.tile_pool(name="shared", bufs=1))
        psum = ctx.enter_context(tc.psum_pool(name="psum", bufs=1))

        offs_sb = keep.tile([P, S // 16], U16, name="offs_sb")
        pos_sb = keep.tile([P, S // 16], U16, name="pos_sb")
        words = keep.tile([P, T], U16, name="words", align_bytes=64)
        scales = keep.tile([P, T], U8, name="scales", align_bytes=64)
        lam_cols = keep.tile([P, NB], F32, name="lam_cols")
        ident = keep.tile([P, P], F32, name="ident", align_bytes=64)

        nc.vector.memset(scales[:].bitcast(I32), 0)
        zeros = keep.tile([P, P], F32, name="zeros")
        nc.vector.memset(zeros[:], 0.0)
        nc.gpsimd.affine_select(
            out=ident[:], in_=zeros[:], pattern=[[-1, P]], compare_op=mybir.AluOpType.not_equal, fill=1.0, base=0, channel_multiplier=1
        )

        nc.sync.dma_start(words[:].bitcast(I32), x_words[0].bitcast(I32))
        nc.sync.dma_start(offs_sb[:], offs)
        for r in range(4):
            nc.sync.dma_start(scales[r:P:32, :].bitcast(I32), x_scales[0, r:16:4, :].bitcast(I32))
        w2_raw = loads.tile([P, 4, N], F32, name="w2_raw", offset=0)
        raw = loads.tile([P, 4 * H + S], F32, name="raw", offset=4 * 4 * N)
        w1_raw = raw[:, 0 : 4 * H].rearrange("p (j c) -> p j c", j=4)
        mu_sb = raw[:, 4 * H :]
        w1_rows = w1.rearrange("(p j) c -> p (j c)", j=4)
        for part in range(2):
            nc.sync.dma_start(raw[:, 2 * H * part : 2 * H * (part + 1)], w1_rows[:, 2 * H * part : 2 * H * (part + 1)])
        nc.sync.dma_start(pos_sb[:], pos1)
        w2_rows = w2.rearrange("(a t e) n -> e a t n", t=4, e=2)
        for e in range(2):
            nc.sync.dma_start(w2_raw[e:P:2], w2_rows[e])
        nc.sync.dma_start(mu_sb, mu)
        with nc.allow_non_contiguous_dma(reason="one share a partition and block"):
            nc.sync.dma_start(lam_cols[:], lam[0].rearrange("(b p) -> p b", p=P))

        x_codes = keep.tile([P, S], U16, name="x_codes", align_bytes=64)
        x_scale = keep.tile([P, S], U8, name="x_scale", align_bytes=64)
        nc.vector.tensor_copy(x_codes[:], words[:].indirect(offs_sb[:]))
        nc.vector.tensor_copy(x_scale[:], scales[:].indirect(offs_sb[:]))

        w1_bf = [keep.tile([P, 4 * P], BF16, name="w1_bf%d" % t, tag="w1_bf%d" % t, align_bytes=64) for t in range(4)]
        w1_codes = keep.tile([P, 4 * P], U32, name="w1_codes", align_bytes=64)
        w1_scale = keep.tile([P, 4 * P], U8, name="w1_scale", align_bytes=64)
        h_sb = [keep.tile([P, S + SPARE if t < 3 else S], F32, name="h_sb%d" % t, align_bytes=64) for t in range(4)]
        for t in range(3):
            nc.scalar.copy(h_sb[t][:, S:], zeros[:, 0:SPARE])
        partner = keep.tile([P, 4, S], F32, name="partner", align_bytes=64)

        def cast_w1(t, rows, copy):
            src = w1_raw.rearrange("p j (a t e) -> p t a j e", t=4, e=2)[:, t, :, rows]
            copy(w1_bf[t][:].rearrange("p (a e j) -> p a j e", e=2, j=4)[:, :, rows], src)

        def quantize_w1(t, staged):
            cols = slice(P * t, P * (t + 1))
            nc.vector.quantize_mx(out=w1_codes[:, cols].bitcast(FP8X4), scales=w1_scale[:, cols], in_=staged)

        def first_product(t, cols, tag):
            bank = psum.tile([P, cols.stop - cols.start], F32, name="h_ps%d_%d" % (t, cols.start), tag=tag)
            nc.tensor.matmul_mx(
                out=bank[:],
                lhsT=w1_codes[:, P * t : P * (t + 1)].bitcast(FP8X4),
                lhsT_scale=w1_scale[:, P * t : P * (t + 1)],
                rhs=x_codes[:, cols].bitcast(FP4X4),
                rhs_scale=x_scale[:, cols],
                start=True,
                stop=True,
            )
            nc.scalar.copy(h_sb[t][:, cols], bank[:])

        for t in range(3):
            cast_w1(t, slice(0, 2), nc.scalar.copy)
        cast_w1(0, slice(2, 4), nc.vector.tensor_copy)
        quantize_w1(0, w1_bf[0][:])
        cast_w1(1, slice(2, 4), nc.vector.tensor_copy)
        cast_w1(2, slice(2, 4), nc.scalar.copy)
        cast_w1(3, slice(0, 4), nc.scalar.copy)
        quantize_w1(1, w1_bf[1][:])
        quantize_w1(2, w1_bf[2][:])
        w2_bf = keep.tile([P, 4 * N], BF16, name="w2_bf", tag="w1_bf1", align_bytes=64)
        w2_codes = keep.tile([P, N], U32, name="w2_codes", align_bytes=64)
        w2_scale = keep.tile([P, N], U8, name="w2_scale", align_bytes=64)
        nc.vector.tensor_copy(
            w2_bf[:].rearrange("p (a e j) -> p a j e", e=4, j=4),
            w2_raw[:].rearrange("p j (a e) -> p a j e", e=4),
        )
        quantize_w1(3, w1_bf[3][:])
        nc.vector.quantize_mx(out=w2_codes[:].bitcast(FP8X4), scales=w2_scale[:], in_=w2_bf[:])
        first_product(0, slice(0, HALF), "a0")
        first_product(0, slice(HALF, S), "a1")
        first_product(1, slice(0, S), "a2")
        for b in range(NB):
            first_product(2 + b // 2, slice(HALF * (b % 2), HALF * (b % 2 + 1)), "t%d" % b)

        ht_ps = [psum.tile([P, 4, P], F32, name="ht_ps%d" % b, tag="t%d" % b) for b in range(NB)]
        for b in range(NB):
            for t in range(4):
                nc.tensor.transpose(ht_ps[b][:, t, :], h_sb[t][:, P * b : P * (b + 1)], ident[:])
        own_first = shared.tile([P, 4, P], F32, name="own_first", align_bytes=64, offset=0)
        own_ps = [psum.tile([P, 4, P], F32, name="own_ps%d" % b, tag="a%d" % b) for b in range(NB)]
        for b in range(NB):
            own_t = shared.tile([P, 4, P], F32, name="own_t%d" % b, align_bytes=64, offset=16 * P * (3 - b % 3))
            nc.scalar.activation(own_t[:], ht_ps[b][:], COPY, scale=lam_cols[:, b : b + 1])
            for t in range(4):
                nc.tensor.transpose(own_ps[b][:, t, :], own_t[:, t, :], ident[:])
            if b == 1:
                nc.scalar.copy(own_first[:], own_ps[0][:])

        for t in range(3):
            nc.vector.tensor_tensor(partner[:, t, :], h_sb[t][:].indirect(pos_sb[:]), mu_sb, MULT)
        for half in range(2):
            cols = slice(HALF * half, HALF * (half + 1))
            nc.vector.tensor_tensor(partner[:, 3, cols], h_sb[3][:].indirect(pos_sb[:, 16 * half : 16 * (half + 1)]), mu_sb[:, cols], MULT)

        z_bf = keep.tile([P, 4 * S], BF16, name="z_bf", align_bytes=64)

        def mix(cols, add, own):
            add(
                z_bf[:, 4 * cols.start : 4 * cols.stop].rearrange("p (q i t) -> p q t i", i=2, t=4),
                own.rearrange("p t (q i) -> p q t i", i=2),
                partner[:, :, cols].rearrange("p t (q i) -> p q t i", i=2),
                ADD,
            )

        z_side = keep.tile([P, 4, P], F32, name="z_side", align_bytes=64)
        nc.gpsimd.tensor_tensor(z_side[:], own_first[:], partner[:, :, 0:P], ADD)
        nc.scalar.copy(
            z_bf[:, 0 : 4 * P].rearrange("p (q i t) -> p q t i", i=2, t=4),
            z_side[:].rearrange("p t (q i) -> p q t i", i=2),
        )
        for b in (1, 2):
            mix(slice(P * b, P * (b + 1)), nc.vector.tensor_tensor, own_ps[b][:])

        z_words = shared.tile([P, S], U32, name="z_words", align_bytes=64, offset=8 * P)
        z_scale = keep.tile([P, S], U8, name="z_scale", align_bytes=64)

        res = keep.tile([P, S], F32, name="res", align_bytes=64)

        def second_product(b, tag, copy):
            cols = slice(P * b, P * (b + 1))
            nc.vector.quantize_mx(out=z_words[:, cols].bitcast(FP8X4), scales=z_scale[:, cols], in_=z_bf[:, 4 * cols.start : 4 * cols.stop])
            out_ps = psum.tile([P, P], F32, name="out_ps%d" % b, tag=tag)
            nc.tensor.matmul_mx(
                out=out_ps[:],
                lhsT=w2_codes[:].bitcast(FP8X4),
                lhsT_scale=w2_scale[:],
                rhs=z_words[:, cols].bitcast(FP8X4),
                rhs_scale=z_scale[:, cols],
                start=True,
                stop=True,
            )
            copy(res[:, cols], out_ps[:])

        second_product(1, "t3", nc.scalar.copy)
        second_product(2, "t1", nc.scalar.copy)
        nc.sync.dma_start(out[:, P : 3 * P], res[:, P : 3 * P])
        mix(slice(3 * P, S), nc.vector.tensor_tensor, own_ps[3][:])
        second_product(0, "t2", nc.scalar.copy)
        nc.sync.dma_start(out[:, 0:P], res[:, 0:P])
        second_product(3, "t0", nc.vector.tensor_copy)
        nc.sync.dma_start(out[:, 3 * P :], res[:, 3 * P :])
